import numpy as np
import ml_dtypes


def mxq(x, axis, fmt="e4m3"):
    dtype, down = {"e4m3": (ml_dtypes.float8_e4m3fn, 7), "e5m2": (ml_dtypes.float8_e5m2, 14)}[fmt]
    v = np.moveaxis(np.asarray(x, np.float32).astype(ml_dtypes.bfloat16).astype(np.float64), axis, -1)
    blocks = v.reshape(v.shape[:-1] + (-1, 32))
    amax = np.abs(blocks).max(-1, keepdims=True)
    byte = np.maximum(np.where(amax > 0, np.frexp(amax)[1] - 1 + 127, 0) - down, 1)
    scale = np.exp2(byte - 127.0)
    codes = (blocks / scale).astype(np.float32).astype(dtype).astype(np.float64)
    return np.moveaxis((codes * scale).reshape(v.shape), -1, axis)


WIDE = False


def mx_kscale(k):
    if not WIDE:
        return np.ones(k)
    levels = np.array([10, -10, 5, -5, 0])
    if k % 512:
        return np.exp2(np.random.permutation(np.resize(levels, k // 32))).repeat(32)
    a = np.empty((k // 512, 16))
    for p in range(k // 512):
        a[p, :8] = np.random.permutation(np.resize(levels, 8))
        for g in range(8):
            far = levels[np.abs(levels - a[p, g]) >= 10]
            a[p, g + 8] = far[np.random.randint(len(far))]
    return np.exp2(a.ravel()).repeat(32)


def f64(x):
    return np.asarray(x).astype(np.float64)


def striped(idx):
    return np.tile(idx.reshape(-1, 16).T, (8, 1)).astype(np.uint16)


def unstriped(offs):
    return offs[:16].T.reshape(-1).astype(np.int64)


def silu(v):
    return v / (1.0 + np.exp(-np.maximum(v, -700.0)))


K, T, D, S, V, H, N = 512, 1024, 3, 512, 256, 512, 256


def setup_inputs():
    n = np.random.standard_normal
    s = mx_kscale(K)[:, None]
    u = mx_kscale(H)
    return {
        "xT": (n((K, T)) * s).astype(np.float32),
        "w1": (n((K, H)) / np.sqrt(K) / s * u).astype(np.float32),
        "w2": (n((H, N)) / np.sqrt(H) / u[:, None]).astype(np.float32),
        "gate": np.tile(np.random.uniform(0.2, 1.0, (D, 1, V)) / np.sqrt(D), (1, N, 1)).astype(np.float32),
        "offs": striped(np.random.permutation(T)[:S]),
        "pos1": striped(np.random.permutation(S)[:V]),
        "pos2": striped(np.random.permutation(S)[:V]),
        "pos3": striped(np.random.permutation(S)[:V]),
    }


def reference(xT, w1, w2, gate, offs, pos1, pos2, pos3):
    idx = unstriped(offs)
    xq = mxq(f64(xT)[:, idx], 0, "e4m3")
    h = silu(mxq(f64(w1), 0, "e4m3").T @ xq)
    y = mxq(f64(w2), 0, "e4m3").T @ mxq(h, 0, "e4m3")
    return sum(f64(gate[d]) * y[:, unstriped(p)] for d, p in enumerate((pos1, pos2, pos3)))

@@ -1,0 +1,228 @@
+from contextlib import ExitStack
+
+import concourse.mybir as mybir
+
+K, T, D, S, V, H, N = 512, 1024, 3, 512, 256, 512, 256
+FLOPS = 2 * S * (K * H + H * N) + 2 * D * N * V
+
+F32 = mybir.dt.float32
+BF16 = mybir.dt.bfloat16
+U32 = mybir.dt.uint32
+U16 = mybir.dt.uint16
+U8 = mybir.dt.uint8
+FP8X4 = mybir.dt.float8_e4m3fn_x4
+SILU = mybir.ActivationFunctionType.Silu
+MULT = mybir.AluOpType.mult
+ADD = mybir.AluOpType.add
+
+P = 128
+PACK = 4
+
+
+def tile_picked_sub_mlp_silu_sub_e_kernel(tc, xT, w1, w2, gate, offs, pos1, pos2, pos3, out):
+    nc = tc.nc
+    with ExitStack() as ctx:
+        keep = ctx.enter_context(tc.tile_pool(name="keep", bufs=1))
+        psum = ctx.enter_context(tc.psum_pool(name="psum", bufs=1))
+
+        offs_t = keep.tile([P, S // 16], U16, name="offs_t")
+        pos_t = [keep.tile([P, V // 16], U16, name=f"pos_t{d}") for d in range(D)]
+
+        x_rows = xT.rearrange("(p j) t -> p j t", j=PACK)
+        w1_rows = w1.rearrange("(p j) c -> p j c", j=PACK)
+        w2_rows = w2.rearrange("(p j) n -> p j n", j=PACK)
+        TH = T // 2
+        x_raw = {}
+
+        x_raw0 = keep.tile([P, 2, T], F32, name="x_raw0")
+        nc.sync.dma_start(out=x_raw0[:], in_=x_rows[:, 0:2, :])
+        for h in range(2):
+            x_raw[0, h] = x_raw0[:, :, h * TH : (h + 1) * TH]
+        nc.sync.dma_start(offs_t[:], offs)
+        for h in range(2):
+            x_raw1 = keep.tile([P, 2, TH], F32, name=f"x_raw1{h}")
+            nc.sync.dma_start(out=x_raw1[:], in_=x_rows[:, 2:4, h * TH : (h + 1) * TH])
+            x_raw[1, h] = x_raw1[:]
+        W1_CUTS = [(0, 256), (256, 384), (384, 512)]
+        w1_raw = []
+        for a, b in W1_CUTS:
+            r = keep.tile([P, PACK, b - a], F32, name=f"w1_raw{a}")
+            nc.sync.dma_start(out=r[:], in_=w1_rows[:, :, a:b])
+            w1_raw.append(r)
+        w2_raw = keep.tile([P, PACK, N], F32, name="w2_raw")
+        nc.sync.dma_start(out=w2_raw[:], in_=w2_rows)
+        for d, p in enumerate((pos1, pos2, pos3)):
+            nc.sync.dma_start(pos_t[d][:], p)
+        gate_t = keep.tile([P, 2 * D, V], F32, name="gate_t")
+        nc.sync.dma_start(out=gate_t[:], in_=gate.rearrange("d (h p) v -> p (d h) v", p=P))
+
+        warm = keep.tile([P, 1], F32, name="warm")
+        warm_o = keep.tile([P, 1], F32, name="warm_o")
+        nc.vector.memset(warm[:], 0.0)
+        nc.scalar.activation(warm_o[:], warm[:], SILU)
+
+        x_pair = [keep.tile([P, T, 2], BF16, name=f"x_pair{u}") for u in range(2)]
+        X_VECTOR = {(0, 0): 320, (0, 1): 320, (1, 0): 0, (1, 1): 320}
+
+        def cast_x(u, h):
+            src = x_raw[u, h].rearrange("p e (c i) -> p c e i", i=4)
+            dst = x_pair[u][:, h * TH : (h + 1) * TH, :].rearrange("p (c i) e -> p c e i", i=4)
+            cut = X_VECTOR[u, h] // 4
+            if cut:
+                nc.vector.tensor_copy(out=dst[:, :cut], in_=src[:, :cut])
+            nc.scalar.copy(out=dst[:, cut:], in_=src[:, cut:])
+
+        xg = keep.tile([P, S, PACK], BF16, name="xg", align_bytes=64)
+        xg_words = xg[:].rearrange("p s t -> p (s t)").bitcast(U32).rearrange("p (s u) -> p s u", u=2)
+        x_codes = keep.tile([P, S], U32, name="x_codes", align_bytes=64)
+        x_scales = keep.tile([P, S], U8, name="x_scales", align_bytes=64)
+
+        def gather_x(u, a, b):
+            window = x_pair[u][:].rearrange("p t e -> p (t e)").bitcast(U32)
+            nc.vector.tensor_copy(out=xg_words[:, a:b, u], in_=window.indirect(offs_t[:, a // 16 : b // 16]))
+
+        def quant_x(a, b):
+            nc.vector.quantize_mx(
+                out=x_codes[:, a:b].bitcast(FP8X4),
+                scales=x_scales[:, a:b],
+                in_=xg[:, a:b, :].rearrange("p s t -> p (s t)"),
+            )
+
+        w1g = keep.tile([P, PACK, P, PACK], BF16, name="w1g", align_bytes=64)
+        w1_codes = keep.tile([P, H], U32, name="w1_codes", align_bytes=64)
+        w1_scales = keep.tile([P, H], U8, name="w1_scales", align_bytes=64)
+
+        def cast_w1(i, engine_copy, f0, f1):
+            a, b = W1_CUTS[i]
+            src = w1_raw[i][:].rearrange("p j (m t) -> p m j t", t=PACK)
+            n = (b - a) // PACK
+            m0, m1 = int(n * f0), int(n * f1)
+            engine_copy(
+                out=w1g[:].rearrange("p t m j -> p m j t")[:, a // PACK + m0 : a // PACK + m1],
+                in_=src[:, m0:m1],
+            )
+
+        def quant_w1(half):
+            for t in range(PACK):
+                m0 = half * 64
+                cols = slice(t * P + m0, t * P + m0 + 64)
+                nc.vector.quantize_mx(
+                    out=w1_codes[:, cols].bitcast(FP8X4),
+                    scales=w1_scales[:, cols],
+                    in_=w1g[:, t, m0 : m0 + 64, :].rearrange("p m j -> p (m j)"),
+                )
+
+        cast_x(0, 0)
+        cast_x(0, 1)
+        gather_x(0, 0, S)
+        cast_x(1, 0)
+        cast_x(1, 1)
+        gather_x(1, 0, S // 2)
+        gather_x(1, S // 2, S)
+        cast_w1(0, nc.scalar.copy, 0.0, 1.0)
+        cast_w1(1, nc.scalar.copy, 0.0, 1.0)
+        quant_w1(0)
+        cast_w1(2, nc.vector.tensor_copy, 0.0, 1.0)
+        quant_x(0, 128)
+        quant_w1(1)
+        quant_x(128, 256)
+        quant_x(256, 512)
+
+        w2g = keep.tile([P, N, PACK], BF16, name="w2g", align_bytes=64)
+        w2_codes = keep.tile([P, N], U32, name="w2_codes", align_bytes=64)
+        w2_scales = keep.tile([P, N], U8, name="w2_scales", align_bytes=64)
+        nc.vector.tensor_copy(
+            out=w2g[:].rearrange("p (c i) j -> p c j i", i=4), in_=w2_raw[:].rearrange("p j (c i) -> p c j i", i=4)
+        )
+        nc.vector.quantize_mx(
+            out=w2_codes[:].bitcast(FP8X4), scales=w2_scales[:], in_=w2g[:].rearrange("p n j -> p (n j)")
+        )
+
+        CUTS = [(0, 128), (128, 256), (256, 384), (384, 448), (448, 512)]
+        h_codes = keep.tile([P, S], U32, name="h_codes", align_bytes=64)
+        h_scales = keep.tile([P, S], U8, name="h_scales", align_bytes=64)
+        hg = [keep.tile([P, b - a, PACK], BF16, name=f"hg{a}", align_bytes=64) for a, b in CUTS]
+        y_t = [keep.tile([P, S], F32, name=f"y_t{h}") for h in range(2)]
+
+        def layer1(c):
+            a, b = CUTS[c]
+            ps = psum.tile([P, PACK, b - a], F32, name=f"h_ps{c}", tag=f"h_ps{c % 4}")
+            for t in range(PACK):
+                nc.tensor.matmul_mx(
+                    out=ps[:, t, :],
+                    lhsT=w1_codes[:, t * P : (t + 1) * P].bitcast(FP8X4),
+                    lhsT_scale=w1_scales[:, t * P : (t + 1) * P],
+                    rhs=x_codes[:, a:b].bitcast(FP8X4),
+                    rhs_scale=x_scales[:, a:b],
+                    start=True,
+                    stop=True,
+                )
+            nc.scalar.activation(hg[c][:], ps[:].rearrange("p t s -> p s t"), SILU)
+
+        def quant_h(c):
+            a, b = CUTS[c]
+            nc.vector.quantize_mx(
+                out=h_codes[:, a:b].bitcast(FP8X4),
+                scales=h_scales[:, a:b],
+                in_=hg[c][:].rearrange("p s t -> p (s t)"),
+            )
+
+        def layer2(dst, h, a, b):
+            nc.tensor.matmul_mx(
+                out=dst,
+                lhsT=w2_codes[:, h * P : (h + 1) * P].bitcast(FP8X4),
+                lhsT_scale=w2_scales[:, h * P : (h + 1) * P],
+                rhs=h_codes[:, a:b].bitcast(FP8X4),
+                rhs_scale=h_scales[:, a:b],
+                start=True,
+                stop=True,
+            )
+
+        for c in range(5):
+            layer1(c)
+        y_a = psum.tile([P, 2, 256], F32, name="y_a")
+        y_b = psum.tile([P, 2, 192], F32, name="y_b")
+        y_c = [psum.tile([P, 64], F32, name=f"y_c{h}") for h in range(2)]
+        quant_h(0)
+        quant_h(1)
+        for h in range(2):
+            layer2(y_a[:, h, :], h, 0, 256)
+        quant_h(2)
+        for h in range(2):
+            layer2(y_b[:, h, 0:128], h, 256, 384)
+        for h in range(2):
+            nc.vector.tensor_copy(out=y_t[h][:, 0:256], in_=y_a[:, h, :])
+        quant_h(3)
+        for h in range(2):
+            layer2(y_b[:, h, 128:192], h, 384, 448)
+        quant_h(4)
+        for h in (1, 0):
+            layer2(y_c[h][:], h, 448, 512)
+        for h in range(2):
+            nc.vector.tensor_copy(out=y_t[h][:, 256:448], in_=y_b[:, h, :])
+        nc.vector.tensor_copy(out=y_t[1][:, 448:512], in_=y_c[1][:])
+        nc.scalar.copy(out=y_t[0][:, 448:512], in_=y_c[0][:])
+
+        prod = [keep.tile([P, 2, V], F32, name=f"prod{d}") for d in range(D)]
+
+        def fetch(h, d):
+            nc.vector.tensor_tensor(
+                prod[d][:, h, :], y_t[h][:].indirect(pos_t[d][:]), gate_t[:, 2 * d + h, :], MULT
+            )
+
+        fetch(1, 0)
+        fetch(0, 0)
+        fetch(1, 1)
+        fetch(0, 1)
+        fetch(1, 2)
+        part = keep.tile([P, 2, V], F32, name="part")
+        nc.vector.tensor_tensor(part[:], prod[0][:], prod[1][:], ADD)
+        fetch(0, 2)
+        res1 = keep.tile([P, V], F32, name="res1")
+        nc.vector.tensor_tensor(res1[:], part[:, 1, :], prod[2][:, 1, :], ADD)
+        nc.sync.dma_start(out=out[P : 2 * P, :], in_=res1[:])
+        for q in range(2):
+            cols = slice(q * V // 2, (q + 1) * V // 2)
+            res0 = keep.tile([P, V // 2], F32, name=f"res0{q}")
+            nc.vector.tensor_tensor(res0[:], part[:, 0, cols], prod[2][:, 0, cols], ADD)
+            nc.sync.dma_start(out=out[0:P, cols], in_=res0[:])

@@ -1,12 +1,14 @@
 from contextlib import ExitStack
 
 import concourse.mybir as mybir
+from concourse.masks import make_identity
 
 K, T, D, S, V, H, N = 512, 1024, 3, 512, 256, 512, 256
 FLOPS = 2 * S * (K * H + H * N) + 2 * D * N * V
 
 F32 = mybir.dt.float32
 BF16 = mybir.dt.bfloat16
+I32 = mybir.dt.int32
 U32 = mybir.dt.uint32
 U16 = mybir.dt.uint16
 U8 = mybir.dt.uint8
@@ -31,112 +33,111 @@ def tile_picked_sub_mlp_silu_sub_e_kernel(tc, xT, w1, w2, gate, offs, pos1, pos2
         x_rows = xT.rearrange("(p j) t -> p j t", j=PACK)
         w1_rows = w1.rearrange("(p j) c -> p j c", j=PACK)
         w2_rows = w2.rearrange("(p j) n -> p j n", j=PACK)
-        TH = T // 2
-        x_raw = {}
 
+        X1_CUT = 512
         x_raw0 = keep.tile([P, 2, T], F32, name="x_raw0")
         nc.sync.dma_start(out=x_raw0[:], in_=x_rows[:, 0:2, :])
-        for h in range(2):
-            x_raw[0, h] = x_raw0[:, :, h * TH : (h + 1) * TH]
         nc.sync.dma_start(offs_t[:], offs)
-        for h in range(2):
-            x_raw1 = keep.tile([P, 2, TH], F32, name=f"x_raw1{h}")
-            nc.sync.dma_start(out=x_raw1[:], in_=x_rows[:, 2:4, h * TH : (h + 1) * TH])
-            x_raw[1, h] = x_raw1[:]
-        W1_CUTS = [(0, 256), (256, 384), (384, 512)]
-        w1_raw = []
-        for a, b in W1_CUTS:
-            r = keep.tile([P, PACK, b - a], F32, name=f"w1_raw{a}")
-            nc.sync.dma_start(out=r[:], in_=w1_rows[:, :, a:b])
-            w1_raw.append(r)
+        x_raw1a = keep.tile([P, 2, X1_CUT], F32, name="x_raw1a")
+        nc.sync.dma_start(out=x_raw1a[:], in_=x_rows[:, 2:4, 0:X1_CUT])
+        x_raw1b = keep.tile([P, 2, T - X1_CUT], F32, name="x_raw1b")
+        nc.sync.dma_start(out=x_raw1b[:], in_=x_rows[:, 2:4, X1_CUT:T])
+        HH = H // 2
+        w1_a = keep.tile([P, PACK, HH], F32, name="w1_a")
+        nc.sync.dma_start(out=w1_a[:], in_=w1_rows[:, :, 0:HH])
+        w1_b = keep.tile([P, PACK, HH], F32, name="w1_b", tag="w1_b", align_bytes=64)
+        nc.sync.dma_start(out=w1_b[:], in_=w1_rows[:, :, HH:H])
         w2_raw = keep.tile([P, PACK, N], F32, name="w2_raw")
         nc.sync.dma_start(out=w2_raw[:], in_=w2_rows)
         for d, p in enumerate((pos1, pos2, pos3)):
             nc.sync.dma_start(pos_t[d][:], p)
-        gate_t = keep.tile([P, 2 * D, V], F32, name="gate_t")
-        nc.sync.dma_start(out=gate_t[:], in_=gate.rearrange("d (h p) v -> p (d h) v", p=P))
+        gate_t = keep.tile([P, D, V], F32, name="gate_t")
+        nc.sync.dma_start(out=gate_t[:], in_=gate[:, 0:P, :].rearrange("d p v -> p d v"))
 
         warm = keep.tile([P, 1], F32, name="warm")
         warm_o = keep.tile([P, 1], F32, name="warm_o")
         nc.vector.memset(warm[:], 0.0)
         nc.scalar.activation(warm_o[:], warm[:], SILU)
+        ident = keep.tile([P, P], F32, name="ident")
+        make_identity(nc, ident[:])
 
         x_pair = [keep.tile([P, T, 2], BF16, name=f"x_pair{u}") for u in range(2)]
-        X_VECTOR = {(0, 0): 320, (0, 1): 320, (1, 0): 0, (1, 1): 320}
 
-        def cast_x(u, h):
-            src = x_raw[u, h].rearrange("p e (c i) -> p c e i", i=4)
-            dst = x_pair[u][:, h * TH : (h + 1) * TH, :].rearrange("p (c i) e -> p c e i", i=4)
-            cut = X_VECTOR[u, h] // 4
+        def cast_x(u, raw, t0, n, n_vec):
+            src = raw.rearrange("p e (c i) -> p c e i", i=4)
+            dst = x_pair[u][:, t0 : t0 + n, :].rearrange("p (c i) e -> p c e i", i=4)
+            cut = n_vec // 4
             if cut:
                 nc.vector.tensor_copy(out=dst[:, :cut], in_=src[:, :cut])
             nc.scalar.copy(out=dst[:, cut:], in_=src[:, cut:])
 
-        xg = keep.tile([P, S, PACK], BF16, name="xg", align_bytes=64)
-        xg_words = xg[:].rearrange("p s t -> p (s t)").bitcast(U32).rearrange("p (s u) -> p s u", u=2)
-        x_codes = keep.tile([P, S], U32, name="x_codes", align_bytes=64)
+        picked = keep.tile([P, 2, S], U32, name="picked")
+        x_codes = [keep.tile([P, S // 2], U32, name="x_codes_lo", align_bytes=64)]
         x_scales = keep.tile([P, S], U8, name="x_scales", align_bytes=64)
 
         def gather_x(u, a, b):
             window = x_pair[u][:].rearrange("p t e -> p (t e)").bitcast(U32)
-            nc.vector.tensor_copy(out=xg_words[:, a:b, u], in_=window.indirect(offs_t[:, a // 16 : b // 16]))
+            nc.vector.tensor_copy(out=picked[:, u, a:b], in_=window.indirect(offs_t[:, a // 16 : b // 16]))
 
-        def quant_x(a, b):
+        def weave_x(dst, a, b):
+            nc.vector.tensor_copy(
+                out=dst[:].rearrange("p s t -> p (s t)").bitcast(I32).rearrange("p (c i u) -> p c u i", u=2, i=4),
+                in_=picked[:, :, a:b].bitcast(I32).rearrange("p u (c i) -> p c u i", i=4),
+            )
+
+        def quant_x(src, s0, a, b):
             nc.vector.quantize_mx(
-                out=x_codes[:, a:b].bitcast(FP8X4),
+                out=x_codes[s0 // 256][:, a - s0 : b - s0].bitcast(FP8X4),
                 scales=x_scales[:, a:b],
-                in_=xg[:, a:b, :].rearrange("p s t -> p (s t)"),
+                in_=src[:, a - s0 : b - s0, :].rearrange("p s t -> p (s t)"),
             )
 
         w1g = keep.tile([P, PACK, P, PACK], BF16, name="w1g", align_bytes=64)
         w1_codes = keep.tile([P, H], U32, name="w1_codes", align_bytes=64)
         w1_scales = keep.tile([P, H], U8, name="w1_scales", align_bytes=64)
 
-        def cast_w1(i, engine_copy, f0, f1):
-            a, b = W1_CUTS[i]
-            src = w1_raw[i][:].rearrange("p j (m t) -> p m j t", t=PACK)
-            n = (b - a) // PACK
-            m0, m1 = int(n * f0), int(n * f1)
+        def cast_w1(raw, m_base, engine_copy, m0, m1, t0, t1):
+            src = raw[:].rearrange("p j (m t) -> p m j t", t=PACK)
             engine_copy(
-                out=w1g[:].rearrange("p t m j -> p m j t")[:, a // PACK + m0 : a // PACK + m1],
-                in_=src[:, m0:m1],
+                out=w1g[:].rearrange("p t m j -> p m j t")[:, m_base + m0 : m_base + m1, :, t0:t1],
+                in_=src[:, m0:m1, :, t0:t1],
             )
 
-        def quant_w1(half):
-            for t in range(PACK):
-                m0 = half * 64
-                cols = slice(t * P + m0, t * P + m0 + 64)
-                nc.vector.quantize_mx(
-                    out=w1_codes[:, cols].bitcast(FP8X4),
-                    scales=w1_scales[:, cols],
-                    in_=w1g[:, t, m0 : m0 + 64, :].rearrange("p m j -> p (m j)"),
-                )
+        def quant_w1(t):
+            cols = slice(t * P, (t + 1) * P)
+            nc.vector.quantize_mx(
+                out=w1_codes[:, cols].bitcast(FP8X4),
+                scales=w1_scales[:, cols],
+                in_=w1g[:, t, :, :].rearrange("p m j -> p (m j)"),
+            )
 
-        cast_x(0, 0)
-        cast_x(0, 1)
+        cast_x(0, x_raw0[:], 0, T, 688)
         gather_x(0, 0, S)
-        cast_x(1, 0)
-        cast_x(1, 1)
-        gather_x(1, 0, S // 2)
-        gather_x(1, S // 2, S)
-        cast_w1(0, nc.scalar.copy, 0.0, 1.0)
-        cast_w1(1, nc.scalar.copy, 0.0, 1.0)
-        quant_w1(0)
-        cast_w1(2, nc.vector.tensor_copy, 0.0, 1.0)
-        quant_x(0, 128)
-        quant_w1(1)
-        quant_x(128, 256)
-        quant_x(256, 512)
+        cast_x(1, x_raw1a[:], 0, X1_CUT, 0)
+        cast_x(1, x_raw1b[:], X1_CUT, T - X1_CUT, 400)
+        xg_lo = keep.tile([P, S // 2, PACK], BF16, name="xg_lo", align_bytes=64)
+        xg_hi = keep.tile([P, S // 2, PACK], BF16, name="xg_hi", align_bytes=64)
+        gather_x(1, 0, 256)
+        gather_x(1, 256, 512)
+        weave_x(xg_lo, 0, 256)
+        weave_x(xg_hi, 256, 512)
+        quant_x(xg_lo, 0, 0, 256)
+        cast_w1(w1_a, 0, nc.scalar.copy, 0, 64, 0, 4)
+        cast_w1(w1_b, 64, nc.scalar.copy, 0, 64, 0, 2)
+        cast_w1(w1_b, 64, nc.vector.tensor_copy, 0, 40, 2, 4)
+        cast_w1(w1_b, 64, nc.scalar.copy, 40, 64, 2, 4)
+        for t in range(PACK):
+            quant_w1(t)
+        x_codes.append(keep.tile([P, S // 2], U32, name="x_codes_hi", tag="w1_b", align_bytes=64))
+        quant_x(xg_hi, 256, 256, 384)
+        quant_x(xg_hi, 256, 384, 512)
 
         w2g = keep.tile([P, N, PACK], BF16, name="w2g", align_bytes=64)
         w2_codes = keep.tile([P, N], U32, name="w2_codes", align_bytes=64)
         w2_scales = keep.tile([P, N], U8, name="w2_scales", align_bytes=64)
-        nc.vector.tensor_copy(
-            out=w2g[:].rearrange("p (c i) j -> p c j i", i=4), in_=w2_raw[:].rearrange("p j (c i) -> p c j i", i=4)
-        )
-        nc.vector.quantize_mx(
-            out=w2_codes[:].bitcast(FP8X4), scales=w2_scales[:], in_=w2g[:].rearrange("p n j -> p (n j)")
-        )
+        w2g_v = w2g[:].rearrange("p (c i) j -> p c j i", i=4)
+        w2_v = w2_raw[:].rearrange("p j (c i) -> p c j i", i=4)
+        nc.vector.tensor_copy(out=w2g_v, in_=w2_v)
 
         CUTS = [(0, 128), (128, 256), (256, 384), (384, 448), (448, 512)]
         h_codes = keep.tile([P, S], U32, name="h_codes", align_bytes=64)
@@ -145,19 +146,21 @@ def tile_picked_sub_mlp_silu_sub_e_kernel(tc, xT, w1, w2, gate, offs, pos1, pos2
         y_t = [keep.tile([P, S], F32, name=f"y_t{h}") for h in range(2)]
 
         def layer1(c):
-            a, b = CUTS[c]
-            ps = psum.tile([P, PACK, b - a], F32, name=f"h_ps{c}", tag=f"h_ps{c % 4}")
+            a, b = c * P, (c + 1) * P
+            ps = psum.tile([P, PACK, P], F32, name=f"h_ps{c}", tag=f"bank{c}")
             for t in range(PACK):
                 nc.tensor.matmul_mx(
                     out=ps[:, t, :],
                     lhsT=w1_codes[:, t * P : (t + 1) * P].bitcast(FP8X4),
                     lhsT_scale=w1_scales[:, t * P : (t + 1) * P],
-                    rhs=x_codes[:, a:b].bitcast(FP8X4),
+                    rhs=x_codes[c // 2][:, (c % 2) * P : (c % 2 + 1) * P].bitcast(FP8X4),
                     rhs_scale=x_scales[:, a:b],
                     start=True,
                     stop=True,
                 )
-            nc.scalar.activation(hg[c][:], ps[:].rearrange("p t s -> p s t"), SILU)
+            for i, (s0, s1) in enumerate(CUTS):
+                if a <= s0 < b:
+                    nc.scalar.activation(hg[i][:], ps[:, :, s0 - a : s1 - a].rearrange("p t s -> p s t"), SILU)
 
         def quant_h(c):
             a, b = CUTS[c]
@@ -178,51 +181,61 @@ def tile_picked_sub_mlp_silu_sub_e_kernel(tc, xT, w1, w2, gate, offs, pos1, pos2
                 stop=True,
             )
 
-        for c in range(5):
+        for c in range(4):
             layer1(c)
-        y_a = psum.tile([P, 2, 256], F32, name="y_a")
-        y_b = psum.tile([P, 2, 192], F32, name="y_b")
-        y_c = [psum.tile([P, 64], F32, name=f"y_c{h}") for h in range(2)]
+        y_main = [psum.tile([P, 384], F32, name=f"y_main{h}", tag=f"bank{4 + h}") for h in range(2)]
+        ya_last = [psum.tile([P, 64], F32, name=f"ya_last{q}", tag=f"bank{6 + q}") for q in range(2)]
+        yb_last = psum.tile([P, 128], F32, name="yb_last", tag="bank0")
         quant_h(0)
+        nc.vector.quantize_mx(
+            out=w2_codes[:].bitcast(FP8X4), scales=w2_scales[:], in_=w2g[:].rearrange("p n j -> p (n j)")
+        )
         quant_h(1)
         for h in range(2):
-            layer2(y_a[:, h, :], h, 0, 256)
+            layer2(y_main[h][:, 0:256], h, 0, 256)
         quant_h(2)
         for h in range(2):
-            layer2(y_b[:, h, 0:128], h, 256, 384)
-        for h in range(2):
-            nc.vector.tensor_copy(out=y_t[h][:, 0:256], in_=y_a[:, h, :])
+            layer2(y_main[h][:, 256:384], h, 256, 384)
         quant_h(3)
-        for h in range(2):
-            layer2(y_b[:, h, 128:192], h, 384, 448)
+        layer2(ya_last[0][:], 0, 384, 448)
         quant_h(4)
-        for h in (1, 0):
-            layer2(y_c[h][:], h, 448, 512)
-        for h in range(2):
-            nc.vector.tensor_copy(out=y_t[h][:, 256:448], in_=y_b[:, h, :])
-        nc.vector.tensor_copy(out=y_t[1][:, 448:512], in_=y_c[1][:])
-        nc.scalar.copy(out=y_t[0][:, 448:512], in_=y_c[0][:])
+        layer2(ya_last[1][:], 0, 448, 512)
+        layer2(yb_last[:], 1, 384, 512)
+        nc.scalar.copy(out=y_t[0][:, 0:384], in_=y_main[0][:])
+        nc.scalar.copy(out=y_t[0][:, 384:448], in_=ya_last[0][:])
+        nc.scalar.copy(out=y_t[0][:, 448:512], in_=ya_last[1][:])
+        nc.scalar.copy(out=y_t[1][:, 0:384], in_=y_main[1][:])
+        nc.scalar.copy(out=y_t[1][:, 384:512], in_=yb_last[:])
 
-        prod = [keep.tile([P, 2, V], F32, name=f"prod{d}") for d in range(D)]
+        def fetch(dst, h, d, a, b):
+            nc.vector.tensor_tensor(dst, y_t[h][:].indirect(pos_t[d][:, a // 16 : b // 16]), gate_t[:, d, a:b], MULT)
 
-        def fetch(h, d):
-            nc.vector.tensor_tensor(
-                prod[d][:, h, :], y_t[h][:].indirect(pos_t[d][:]), gate_t[:, 2 * d + h, :], MULT
-            )
-
-        fetch(1, 0)
-        fetch(0, 0)
-        fetch(1, 1)
-        fetch(0, 1)
-        fetch(1, 2)
-        part = keep.tile([P, 2, V], F32, name="part")
-        nc.vector.tensor_tensor(part[:], prod[0][:], prod[1][:], ADD)
-        fetch(0, 2)
-        res1 = keep.tile([P, V], F32, name="res1")
-        nc.vector.tensor_tensor(res1[:], part[:, 1, :], prod[2][:, 1, :], ADD)
-        nc.sync.dma_start(out=out[P : 2 * P, :], in_=res1[:])
+        prod_a = [keep.tile([P, V], F32, name=f"prod_a{d}") for d in range(D)]
+        prod_b = [keep.tile([P, V], F32, name=f"prod_b{d}") for d in range(D)]
+        sum_t = [psum.tile([P, P], F32, name=f"sum_t{q}", tag=f"bank{1 + q}") for q in range(2)]
+        for d in range(D):
+            fetch(prod_a[d][:], 0, d, 0, V)
+            for q in range(2):
+                nc.tensor.matmul(
+                    sum_t[q][:], prod_a[d][:, q * P : (q + 1) * P], ident[:], start=(d == 0), stop=(d == D - 1), is_transpose=True
+                )
+        sum_sb = [keep.tile([P, P], F32, name=f"sum_sb{q}") for q in range(2)]
+        back = psum.tile([P, V], F32, name="back", tag="bank3")
         for q in range(2):
-            cols = slice(q * V // 2, (q + 1) * V // 2)
-            res0 = keep.tile([P, V // 2], F32, name=f"res0{q}")
-            nc.vector.tensor_tensor(res0[:], part[:, 0, cols], prod[2][:, 0, cols], ADD)
-            nc.sync.dma_start(out=out[0:P, cols], in_=res0[:])
+            nc.scalar.copy(out=sum_sb[q][:], in_=sum_t[q][:])
+            nc.tensor.transpose(back[:, q * P : (q + 1) * P], sum_sb[q][:], ident[:])
+        res_a = keep.tile([P, V], F32, name="res_a")
+        nc.scalar.copy(out=res_a[:], in_=back[:])
+        nc.scalar.dma_start(out=out[0:P, :], in_=res_a[:])
+
+        fetch(prod_b[0][:], 1, 0, 0, V)
+        fetch(prod_b[1][:], 1, 1, 0, V)
+        fetch(prod_b[2][:, 0:P], 1, 2, 0, P)
+        part = keep.tile([P, V], F32, name="part")
+        nc.vector.tensor_tensor(part[:], prod_b[0][:], prod_b[1][:], ADD)
+        fetch(prod_b[2][:, P:V], 1, 2, P, V)
+        for q in range(2):
+            cols = slice(q * P, (q + 1) * P)
+            res_b = keep.tile([P, P], F32, name=f"res_b{q}")
+            nc.vector.tensor_tensor(res_b[:], part[:, cols], prod_b[2][:, cols], ADD)
+            nc.sync.dma_start(out=out[P : 2 * P, cols], in_=res_b[:])

@@ -35,8 +35,11 @@ def tile_picked_sub_mlp_silu_sub_e_kernel(tc, xT, w1, w2, gate, offs, pos1, pos2
         w2_rows = w2.rearrange("(p j) n -> p j n", j=PACK)
 
         X1_CUT = 512
-        x_raw0 = keep.tile([P, 2, T], F32, name="x_raw0")
-        nc.sync.dma_start(out=x_raw0[:], in_=x_rows[:, 0:2, :])
+        X0_CUT = 704
+        x_raw0a = keep.tile([P, 2, X0_CUT], F32, name="x_raw0a")
+        nc.sync.dma_start(out=x_raw0a[:], in_=x_rows[:, 0:2, 0:X0_CUT])
+        x_raw0b = keep.tile([P, 2, T - X0_CUT], F32, name="x_raw0b")
+        nc.sync.dma_start(out=x_raw0b[:], in_=x_rows[:, 0:2, X0_CUT:T])
         nc.sync.dma_start(offs_t[:], offs)
         x_raw1a = keep.tile([P, 2, X1_CUT], F32, name="x_raw1a")
         nc.sync.dma_start(out=x_raw1a[:], in_=x_rows[:, 2:4, 0:X1_CUT])
@@ -72,22 +75,22 @@ def tile_picked_sub_mlp_silu_sub_e_kernel(tc, xT, w1, w2, gate, offs, pos1, pos2
             nc.scalar.copy(out=dst[:, cut:], in_=src[:, cut:])
 
         picked = keep.tile([P, 2, S], U32, name="picked")
-        x_codes = [keep.tile([P, S // 2], U32, name="x_codes_lo", align_bytes=64)]
+        x_codes = keep.tile([P, S], U32, name="x_codes", align_bytes=64)
         x_scales = keep.tile([P, S], U8, name="x_scales", align_bytes=64)
 
         def gather_x(u, a, b):
             window = x_pair[u][:].rearrange("p t e -> p (t e)").bitcast(U32)
             nc.vector.tensor_copy(out=picked[:, u, a:b], in_=window.indirect(offs_t[:, a // 16 : b // 16]))
 
-        def weave_x(dst, a, b):
-            nc.vector.tensor_copy(
-                out=dst[:].rearrange("p s t -> p (s t)").bitcast(I32).rearrange("p (c i u) -> p c u i", u=2, i=4),
-                in_=picked[:, :, a:b].bitcast(I32).rearrange("p u (c i) -> p c u i", i=4),
+        def weave_x(engine_copy, word, dst, a, b):
+            engine_copy(
+                out=dst.rearrange("p s t -> p (s t)").bitcast(word).rearrange("p (c i u) -> p c u i", u=2, i=4),
+                in_=picked[:, :, a:b].bitcast(word).rearrange("p u (c i) -> p c u i", i=4),
             )
 
         def quant_x(src, s0, a, b):
             nc.vector.quantize_mx(
-                out=x_codes[s0 // 256][:, a - s0 : b - s0].bitcast(FP8X4),
+                out=x_codes[:, a:b].bitcast(FP8X4),
                 scales=x_scales[:, a:b],
                 in_=src[:, a - s0 : b - s0, :].rearrange("p s t -> p (s t)"),
             )
@@ -111,24 +114,27 @@ def tile_picked_sub_mlp_silu_sub_e_kernel(tc, xT, w1, w2, gate, offs, pos1, pos2
                 in_=w1g[:, t, :, :].rearrange("p m j -> p (m j)"),
             )
 
-        cast_x(0, x_raw0[:], 0, T, 688)
+        cast_x(0, x_raw0a[:], 0, X0_CUT, 472)
+        cast_x(0, x_raw0b[:], X0_CUT, T - X0_CUT, 216)
         gather_x(0, 0, S)
         cast_x(1, x_raw1a[:], 0, X1_CUT, 0)
-        cast_x(1, x_raw1b[:], X1_CUT, T - X1_CUT, 400)
+        cast_x(1, x_raw1b[:], X1_CUT, T - X1_CUT, 360)
         xg_lo = keep.tile([P, S // 2, PACK], BF16, name="xg_lo", align_bytes=64)
-        xg_hi = keep.tile([P, S // 2, PACK], BF16, name="xg_hi", align_bytes=64)
         gather_x(1, 0, 256)
         gather_x(1, 256, 512)
-        weave_x(xg_lo, 0, 256)
-        weave_x(xg_hi, 256, 512)
-        quant_x(xg_lo, 0, 0, 256)
+        for c in range(2):
+            weave_x(nc.vector.tensor_copy, I32, xg_lo[:, c * P : (c + 1) * P, :], c * P, (c + 1) * P)
+        for c in range(2):
+            quant_x(xg_lo, 0, c * P, (c + 1) * P)
         cast_w1(w1_a, 0, nc.scalar.copy, 0, 64, 0, 4)
-        cast_w1(w1_b, 64, nc.scalar.copy, 0, 64, 0, 2)
-        cast_w1(w1_b, 64, nc.vector.tensor_copy, 0, 40, 2, 4)
-        cast_w1(w1_b, 64, nc.scalar.copy, 40, 64, 2, 4)
+        for t0, m_vec in ((0, 32), (2, 48)):
+            cast_w1(w1_b, 64, nc.vector.tensor_copy, 0, m_vec, t0, t0 + 2)
+            cast_w1(w1_b, 64, nc.scalar.copy, m_vec, 64, t0, t0 + 2)
         for t in range(PACK):
             quant_w1(t)
-        x_codes.append(keep.tile([P, S // 2], U32, name="x_codes_hi", tag="w1_b", align_bytes=64))
+        xg_hi = keep.tile([P, S // 2, PACK], BF16, name="xg_hi", tag="w1_b", align_bytes=64)
+        for c in range(2):
+            weave_x(nc.scalar.copy, U32, xg_hi[:, c * P : (c + 1) * P, :], (c + 2) * P, (c + 3) * P)
         quant_x(xg_hi, 256, 256, 384)
         quant_x(xg_hi, 256, 384, 512)
 
@@ -148,12 +154,12 @@ def tile_picked_sub_mlp_silu_sub_e_kernel(tc, xT, w1, w2, gate, offs, pos1, pos2
         def layer1(c):
             a, b = c * P, (c + 1) * P
             ps = psum.tile([P, PACK, P], F32, name=f"h_ps{c}", tag=f"bank{c}")
-            for t in range(PACK):
+            for t in (range(PACK) if c == 0 else reversed(range(PACK))):
                 nc.tensor.matmul_mx(
                     out=ps[:, t, :],
                     lhsT=w1_codes[:, t * P : (t + 1) * P].bitcast(FP8X4),
                     lhsT_scale=w1_scales[:, t * P : (t + 1) * P],
-                    rhs=x_codes[c // 2][:, (c % 2) * P : (c % 2 + 1) * P].bitcast(FP8X4),
+                    rhs=x_codes[:, a:b].bitcast(FP8X4),
                     rhs_scale=x_scales[:, a:b],
                     start=True,
                     stop=True,
@@ -183,29 +189,26 @@ def tile_picked_sub_mlp_silu_sub_e_kernel(tc, xT, w1, w2, gate, offs, pos1, pos2
 
         for c in range(4):
             layer1(c)
-        y_main = [psum.tile([P, 384], F32, name=f"y_main{h}", tag=f"bank{4 + h}") for h in range(2)]
+        ya_main = psum.tile([P, 384], F32, name="ya_main", tag="bank4")
         ya_last = [psum.tile([P, 64], F32, name=f"ya_last{q}", tag=f"bank{6 + q}") for q in range(2)]
-        yb_last = psum.tile([P, 128], F32, name="yb_last", tag="bank0")
+        yb = psum.tile([P, S], F32, name="yb", tag="bank5")
         quant_h(0)
         nc.vector.quantize_mx(
             out=w2_codes[:].bitcast(FP8X4), scales=w2_scales[:], in_=w2g[:].rearrange("p n j -> p (n j)")
         )
         quant_h(1)
-        for h in range(2):
-            layer2(y_main[h][:, 0:256], h, 0, 256)
+        layer2(ya_main[:, 0:256], 0, 0, 256)
         quant_h(2)
-        for h in range(2):
-            layer2(y_main[h][:, 256:384], h, 256, 384)
+        layer2(ya_main[:, 256:384], 0, 256, 384)
         quant_h(3)
         layer2(ya_last[0][:], 0, 384, 448)
         quant_h(4)
         layer2(ya_last[1][:], 0, 448, 512)
-        layer2(yb_last[:], 1, 384, 512)
-        nc.scalar.copy(out=y_t[0][:, 0:384], in_=y_main[0][:])
+        layer2(yb[:], 1, 0, S)
+        nc.scalar.copy(out=y_t[0][:, 0:384], in_=ya_main[:])
         nc.scalar.copy(out=y_t[0][:, 384:448], in_=ya_last[0][:])
         nc.scalar.copy(out=y_t[0][:, 448:512], in_=ya_last[1][:])
-        nc.scalar.copy(out=y_t[1][:, 0:384], in_=y_main[1][:])
-        nc.scalar.copy(out=y_t[1][:, 384:512], in_=yb_last[:])
+        nc.scalar.copy(out=y_t[1][:], in_=yb[:])
 
         def fetch(dst, h, d, a, b):
             nc.vector.tensor_tensor(dst, y_t[h][:].indirect(pos_t[d][:, a // 16 : b // 16]), gate_t[:, d, a:b], MULT)
@@ -230,12 +233,12 @@ def tile_picked_sub_mlp_silu_sub_e_kernel(tc, xT, w1, w2, gate, offs, pos1, pos2
 
         fetch(prod_b[0][:], 1, 0, 0, V)
         fetch(prod_b[1][:], 1, 1, 0, V)
-        fetch(prod_b[2][:, 0:P], 1, 2, 0, P)
+        LAST = 192
+        fetch(prod_b[2][:, 0:LAST], 1, 2, 0, LAST)
         part = keep.tile([P, V], F32, name="part")
         nc.vector.tensor_tensor(part[:], prod_b[0][:], prod_b[1][:], ADD)
-        fetch(prod_b[2][:, P:V], 1, 2, P, V)
-        for q in range(2):
-            cols = slice(q * P, (q + 1) * P)
-            res_b = keep.tile([P, P], F32, name=f"res_b{q}")
+        fetch(prod_b[2][:, LAST:V], 1, 2, LAST, V)
+        for q, cols in enumerate((slice(0, LAST), slice(LAST, V))):
+            res_b = keep.tile([P, cols.stop - cols.start], F32, name=f"res_b{q}")
             nc.vector.tensor_tensor(res_b[:], part[:, cols], prod_b[2][:, cols], ADD)
             nc.sync.dma_start(out=out[P : 2 * P, cols], in_=res_b[:])

@@ -35,11 +35,8 @@ def tile_picked_sub_mlp_silu_sub_e_kernel(tc, xT, w1, w2, gate, offs, pos1, pos2
         w2_rows = w2.rearrange("(p j) n -> p j n", j=PACK)
 
         X1_CUT = 512
-        X0_CUT = 704
-        x_raw0a = keep.tile([P, 2, X0_CUT], F32, name="x_raw0a")
-        nc.sync.dma_start(out=x_raw0a[:], in_=x_rows[:, 0:2, 0:X0_CUT])
-        x_raw0b = keep.tile([P, 2, T - X0_CUT], F32, name="x_raw0b")
-        nc.sync.dma_start(out=x_raw0b[:], in_=x_rows[:, 0:2, X0_CUT:T])
+        x_raw0 = keep.tile([P, 2, T], F32, name="x_raw0")
+        nc.sync.dma_start(out=x_raw0[:], in_=x_rows[:, 0:2, :])
         nc.sync.dma_start(offs_t[:], offs)
         x_raw1a = keep.tile([P, 2, X1_CUT], F32, name="x_raw1a")
         nc.sync.dma_start(out=x_raw1a[:], in_=x_rows[:, 2:4, 0:X1_CUT])
@@ -114,8 +111,7 @@ def tile_picked_sub_mlp_silu_sub_e_kernel(tc, xT, w1, w2, gate, offs, pos1, pos2
                 in_=w1g[:, t, :, :].rearrange("p m j -> p (m j)"),
             )
 
-        cast_x(0, x_raw0a[:], 0, X0_CUT, 472)
-        cast_x(0, x_raw0b[:], X0_CUT, T - X0_CUT, 216)
+        cast_x(0, x_raw0[:], 0, T, 688)
         gather_x(0, 0, S)
         cast_x(1, x_raw1a[:], 0, X1_CUT, 0)
         cast_x(1, x_raw1b[:], X1_CUT, T - X1_CUT, 360)
@@ -127,7 +123,7 @@ def tile_picked_sub_mlp_silu_sub_e_kernel(tc, xT, w1, w2, gate, offs, pos1, pos2
         for c in range(2):
             quant_x(xg_lo, 0, c * P, (c + 1) * P)
         cast_w1(w1_a, 0, nc.scalar.copy, 0, 64, 0, 4)
-        for t0, m_vec in ((0, 32), (2, 48)):
+        for t0, m_vec in ((0, 40), (2, 44)):
             cast_w1(w1_b, 64, nc.vector.tensor_copy, 0, m_vec, t0, t0 + 2)
             cast_w1(w1_b, 64, nc.scalar.copy, m_vec, 64, t0, t0 + 2)
         for t in range(PACK):

@@ -25,6 +25,7 @@ def tile_picked_sub_mlp_silu_sub_e_kernel(tc, xT, w1, w2, gate, offs, pos1, pos2
     nc = tc.nc
     with ExitStack() as ctx:
         keep = ctx.enter_context(tc.tile_pool(name="keep", bufs=1))
+        shared = ctx.enter_context(tc.tile_pool(name="shared", bufs=1))
         psum = ctx.enter_context(tc.psum_pool(name="psum", bufs=1))
 
         offs_t = keep.tile([P, S // 16], U16, name="offs_t")
@@ -45,7 +46,7 @@ def tile_picked_sub_mlp_silu_sub_e_kernel(tc, xT, w1, w2, gate, offs, pos1, pos2
         HH = H // 2
         w1_a = keep.tile([P, PACK, HH], F32, name="w1_a")
         nc.sync.dma_start(out=w1_a[:], in_=w1_rows[:, :, 0:HH])
-        w1_b = keep.tile([P, PACK, HH], F32, name="w1_b", tag="w1_b", align_bytes=64)
+        w1_b = shared.tile([P, PACK, HH], F32, name="w1_b", align_bytes=64, offset=0)
         nc.sync.dma_start(out=w1_b[:], in_=w1_rows[:, :, HH:H])
         w2_raw = keep.tile([P, PACK, N], F32, name="w2_raw")
         nc.sync.dma_start(out=w2_raw[:], in_=w2_rows)
@@ -71,13 +72,16 @@ def tile_picked_sub_mlp_silu_sub_e_kernel(tc, xT, w1, w2, gate, offs, pos1, pos2
                 nc.vector.tensor_copy(out=dst[:, :cut], in_=src[:, :cut])
             nc.scalar.copy(out=dst[:, cut:], in_=src[:, cut:])
 
-        picked = keep.tile([P, 2, S], U32, name="picked")
+        picked = keep.tile([P, 2, S - P], U32, name="picked")
+        xg_lo = keep.tile([P, P, PACK], BF16, name="xg_lo", align_bytes=64)
+        first_words = xg_lo[:].rearrange("p s t -> p (s t)").bitcast(U32).rearrange("p (s u) -> p s u", u=2)
         x_codes = keep.tile([P, S], U32, name="x_codes", align_bytes=64)
         x_scales = keep.tile([P, S], U8, name="x_scales", align_bytes=64)
 
-        def gather_x(u, a, b):
+        def gather_x(u):
             window = x_pair[u][:].rearrange("p t e -> p (t e)").bitcast(U32)
-            nc.vector.tensor_copy(out=picked[:, u, a:b], in_=window.indirect(offs_t[:, a // 16 : b // 16]))
+            nc.vector.tensor_copy(out=first_words[:, :, u], in_=window.indirect(offs_t[:, 0 : P // 16]))
+            nc.vector.tensor_copy(out=picked[:, u, :], in_=window.indirect(offs_t[:, P // 16 : S // 16]))
 
         def weave_x(engine_copy, word, dst, a, b):
             engine_copy(
@@ -112,29 +116,24 @@ def tile_picked_sub_mlp_silu_sub_e_kernel(tc, xT, w1, w2, gate, offs, pos1, pos2
             )
 
         cast_x(0, x_raw0[:], 0, T, 688)
-        gather_x(0, 0, S)
+        gather_x(0)
         cast_x(1, x_raw1a[:], 0, X1_CUT, 0)
-        cast_x(1, x_raw1b[:], X1_CUT, T - X1_CUT, 360)
-        xg_lo = keep.tile([P, S // 2, PACK], BF16, name="xg_lo", align_bytes=64)
-        gather_x(1, 0, 256)
-        gather_x(1, 256, 512)
-        for c in range(2):
-            weave_x(nc.vector.tensor_copy, I32, xg_lo[:, c * P : (c + 1) * P, :], c * P, (c + 1) * P)
-        for c in range(2):
-            quant_x(xg_lo, 0, c * P, (c + 1) * P)
+        cast_x(1, x_raw1b[:], X1_CUT, T - X1_CUT, 312)
+        gather_x(1)
+        quant_x(xg_lo, 0, 0, P)
         cast_w1(w1_a, 0, nc.scalar.copy, 0, 64, 0, 4)
         for t0, m_vec in ((0, 40), (2, 44)):
             cast_w1(w1_b, 64, nc.vector.tensor_copy, 0, m_vec, t0, t0 + 2)
             cast_w1(w1_b, 64, nc.scalar.copy, m_vec, 64, t0, t0 + 2)
         for t in range(PACK):
             quant_w1(t)
-        xg_hi = keep.tile([P, S // 2, PACK], BF16, name="xg_hi", tag="w1_b", align_bytes=64)
-        for c in range(2):
-            weave_x(nc.scalar.copy, U32, xg_hi[:, c * P : (c + 1) * P, :], (c + 2) * P, (c + 3) * P)
-        quant_x(xg_hi, 256, 256, 384)
-        quant_x(xg_hi, 256, 384, 512)
+        xg_hi = [shared.tile([P, P, PACK], BF16, name=f"xg_hi{c}", align_bytes=64, offset=c * 1024) for c in range(3)]
+        for c in range(3):
+            weave_x(nc.scalar.copy, U32, xg_hi[c][:], c * P, (c + 1) * P)
+        for c in range(3):
+            quant_x(xg_hi[c], (c + 1) * P, (c + 1) * P, (c + 2) * P)
 
-        w2g = keep.tile([P, N, PACK], BF16, name="w2g", align_bytes=64)
+        w2g = shared.tile([P, N, PACK], BF16, name="w2g", align_bytes=64, offset=0)
         w2_codes = keep.tile([P, N], U32, name="w2_codes", align_bytes=64)
         w2_scales = keep.tile([P, N], U8, name="w2_scales", align_bytes=64)
         w2g_v = w2g[:].rearrange("p (c i) j -> p c j i", i=4)
@@ -185,7 +184,8 @@ def tile_picked_sub_mlp_silu_sub_e_kernel(tc, xT, w1, w2, gate, offs, pos1, pos2
 
         for c in range(4):
             layer1(c)
-        ya_main = psum.tile([P, 384], F32, name="ya_main", tag="bank4")
+        ya_main = psum.tile([P, 256], F32, name="ya_main", tag="bank4")
+        ya_mid = psum.tile([P, P], F32, name="ya_mid", tag="bank0")
         ya_last = [psum.tile([P, 64], F32, name=f"ya_last{q}", tag=f"bank{6 + q}") for q in range(2)]
         yb = psum.tile([P, S], F32, name="yb", tag="bank5")
         quant_h(0)
@@ -193,15 +193,16 @@ def tile_picked_sub_mlp_silu_sub_e_kernel(tc, xT, w1, w2, gate, offs, pos1, pos2
             out=w2_codes[:].bitcast(FP8X4), scales=w2_scales[:], in_=w2g[:].rearrange("p n j -> p (n j)")
         )
         quant_h(1)
-        layer2(ya_main[:, 0:256], 0, 0, 256)
+        layer2(ya_main[:], 0, 0, 256)
         quant_h(2)
-        layer2(ya_main[:, 256:384], 0, 256, 384)
+        layer2(ya_mid[:], 0, 256, 384)
         quant_h(3)
         layer2(ya_last[0][:], 0, 384, 448)
         quant_h(4)
         layer2(ya_last[1][:], 0, 448, 512)
         layer2(yb[:], 1, 0, S)
-        nc.scalar.copy(out=y_t[0][:, 0:384], in_=ya_main[:])
+        nc.scalar.copy(out=y_t[0][:, 0:256], in_=ya_main[:])
+        nc.scalar.copy(out=y_t[0][:, 256:384], in_=ya_mid[:])
         nc.scalar.copy(out=y_t[0][:, 384:448], in_=ya_last[0][:])
         nc.scalar.copy(out=y_t[0][:, 448:512], in_=ya_last[1][:])
         nc.scalar.copy(out=y_t[1][:], in_=yb[:])

@@ -43,11 +43,8 @@ def tile_picked_sub_mlp_silu_sub_e_kernel(tc, xT, w1, w2, gate, offs, pos1, pos2
         nc.sync.dma_start(out=x_raw1a[:], in_=x_rows[:, 2:4, 0:X1_CUT])
         x_raw1b = keep.tile([P, 2, T - X1_CUT], F32, name="x_raw1b")
         nc.sync.dma_start(out=x_raw1b[:], in_=x_rows[:, 2:4, X1_CUT:T])
-        HH = H // 2
-        w1_a = keep.tile([P, PACK, HH], F32, name="w1_a")
-        nc.sync.dma_start(out=w1_a[:], in_=w1_rows[:, :, 0:HH])
-        w1_b = shared.tile([P, PACK, HH], F32, name="w1_b", align_bytes=64, offset=0)
-        nc.sync.dma_start(out=w1_b[:], in_=w1_rows[:, :, HH:H])
+        w1_b = shared.tile([P, PACK, H], F32, name="w1_b", align_bytes=64, offset=0)
+        nc.sync.dma_start(out=w1_b[:], in_=w1_rows)
         w2_raw = keep.tile([P, PACK, N], F32, name="w2_raw")
         nc.sync.dma_start(out=w2_raw[:], in_=w2_rows)
         for d, p in enumerate((pos1, pos2, pos3)):
@@ -75,23 +72,27 @@ def tile_picked_sub_mlp_silu_sub_e_kernel(tc, xT, w1, w2, gate, offs, pos1, pos2
         picked = keep.tile([P, 2, S - P], U32, name="picked")
         xg_lo = keep.tile([P, P, PACK], BF16, name="xg_lo", align_bytes=64)
         first_words = xg_lo[:].rearrange("p s t -> p (s t)").bitcast(U32).rearrange("p (s u) -> p s u", u=2)
-        x_codes = keep.tile([P, S], U32, name="x_codes", align_bytes=64)
+        x_codes = {c: keep.tile([P, P], U32, name=f"x_codes{c}", align_bytes=64) for c in (0, 2, 3)}
         x_scales = keep.tile([P, S], U8, name="x_scales", align_bytes=64)
 
         def gather_x(u):
             window = x_pair[u][:].rearrange("p t e -> p (t e)").bitcast(U32)
             nc.vector.tensor_copy(out=first_words[:, :, u], in_=window.indirect(offs_t[:, 0 : P // 16]))
-            nc.vector.tensor_copy(out=picked[:, u, :], in_=window.indirect(offs_t[:, P // 16 : S // 16]))
+            if u == 0:
+                nc.vector.tensor_copy(out=picked[:, u, :], in_=window.indirect(offs_t[:, P // 16 : S // 16]))
+            else:
+                nc.vector.tensor_copy(out=picked[:, u, 0:P], in_=window.indirect(offs_t[:, P // 16 : 2 * P // 16]))
+                nc.vector.tensor_copy(out=picked[:, u, P:], in_=window.indirect(offs_t[:, 2 * P // 16 : S // 16]))
 
         def weave_x(engine_copy, word, dst, a, b):
             engine_copy(
-                out=dst.rearrange("p s t -> p (s t)").bitcast(word).rearrange("p (c i u) -> p c u i", u=2, i=4),
-                in_=picked[:, :, a:b].bitcast(word).rearrange("p u (c i) -> p c u i", i=4),
+                out=dst.rearrange("p s t -> p (s t)").bitcast(word).rearrange("p (c i u) -> p c u i", u=2, i=2),
+                in_=picked[:, :, a:b].bitcast(word).rearrange("p u (c i) -> p c u i", i=2),
             )
 
         def quant_x(src, s0, a, b):
             nc.vector.quantize_mx(
-                out=x_codes[:, a:b].bitcast(FP8X4),
+                out=x_codes[a // P][:].bitcast(FP8X4),
                 scales=x_scales[:, a:b],
                 in_=src[:, a - s0 : b - s0, :].rearrange("p s t -> p (s t)"),
             )
@@ -118,20 +119,23 @@ def tile_picked_sub_mlp_silu_sub_e_kernel(tc, xT, w1, w2, gate, offs, pos1, pos2
         cast_x(0, x_raw0[:], 0, T, 688)
         gather_x(0)
         cast_x(1, x_raw1a[:], 0, X1_CUT, 0)
-        cast_x(1, x_raw1b[:], X1_CUT, T - X1_CUT, 312)
+        cast_x(1, x_raw1b[:], X1_CUT, T - X1_CUT, 336)
         gather_x(1)
         quant_x(xg_lo, 0, 0, P)
-        cast_w1(w1_a, 0, nc.scalar.copy, 0, 64, 0, 4)
-        for t0, m_vec in ((0, 40), (2, 44)):
-            cast_w1(w1_b, 64, nc.vector.tensor_copy, 0, m_vec, t0, t0 + 2)
-            cast_w1(w1_b, 64, nc.scalar.copy, m_vec, 64, t0, t0 + 2)
+        xg_1 = keep.tile([P, P, PACK], BF16, name="xg_1", align_bytes=64)
+        weave_x(nc.scalar.copy, U32, xg_1[:], 0, P)
+        for t0, m_vec in ((0, 86), (2, 80)):
+            cast_w1(w1_b, 0, nc.vector.tensor_copy, 0, m_vec, t0, t0 + 2)
+            cast_w1(w1_b, 0, nc.scalar.copy, m_vec, P, t0, t0 + 2)
         for t in range(PACK):
             quant_w1(t)
-        xg_hi = [shared.tile([P, P, PACK], BF16, name=f"xg_hi{c}", align_bytes=64, offset=c * 1024) for c in range(3)]
-        for c in range(3):
-            weave_x(nc.scalar.copy, U32, xg_hi[c][:], c * P, (c + 1) * P)
-        for c in range(3):
-            quant_x(xg_hi[c], (c + 1) * P, (c + 1) * P, (c + 2) * P)
+        xg_hi = [shared.tile([P, P, PACK], BF16, name=f"xg_hi{c}", align_bytes=64, offset=(c + 1) * 1024) for c in range(2)]
+        x_codes[1] = shared.tile([P, P], U32, name="x_codes1", align_bytes=64, offset=3072)
+        quant_x(xg_1, P, P, 2 * P)
+        for c in range(2):
+            weave_x(nc.scalar.copy, U32, xg_hi[c][:], (c + 1) * P, (c + 2) * P)
+        for c in range(2):
+            quant_x(xg_hi[c], (c + 2) * P, (c + 2) * P, (c + 3) * P)
 
         w2g = shared.tile([P, N, PACK], BF16, name="w2g", align_bytes=64, offset=0)
         w2_codes = keep.tile([P, N], U32, name="w2_codes", align_bytes=64)
@@ -154,7 +158,7 @@ def tile_picked_sub_mlp_silu_sub_e_kernel(tc, xT, w1, w2, gate, offs, pos1, pos2
                     out=ps[:, t, :],
                     lhsT=w1_codes[:, t * P : (t + 1) * P].bitcast(FP8X4),
                     lhsT_scale=w1_scales[:, t * P : (t + 1) * P],
-                    rhs=x_codes[:, a:b].bitcast(FP8X4),
+                    rhs=x_codes[c][:].bitcast(FP8X4),
                     rhs_scale=x_scales[:, a:b],
                     start=True,
                     stop=True,

@@ -33,7 +33,7 @@ def tile_picked_sub_mlp_silu_sub_e_kernel(tc, xT, w1, w2, gate, offs, pos1, pos2
 
         x_rows = xT.rearrange("(p j) t -> p j t", j=PACK)
         w1_rows = w1.rearrange("(p j) c -> p j c", j=PACK)
-        w2_rows = w2.rearrange("(p j) n -> p j n", j=PACK)
+        w2_rows = w2.rearrange("(a j e) n -> e a j n", j=PACK, e=2)
 
         X1_CUT = 512
         x_raw0 = keep.tile([P, 2, T], F32, name="x_raw0")
@@ -45,8 +45,9 @@ def tile_picked_sub_mlp_silu_sub_e_kernel(tc, xT, w1, w2, gate, offs, pos1, pos2
         nc.sync.dma_start(out=x_raw1b[:], in_=x_rows[:, 2:4, X1_CUT:T])
         w1_b = shared.tile([P, PACK, H], F32, name="w1_b", align_bytes=64, offset=0)
         nc.sync.dma_start(out=w1_b[:], in_=w1_rows)
-        w2_raw = keep.tile([P, PACK, N], F32, name="w2_raw")
-        nc.sync.dma_start(out=w2_raw[:], in_=w2_rows)
+        w2_raw = shared.tile([P, PACK, N], F32, name="w2_raw", align_bytes=64, offset=8192)
+        for e in range(2):
+            nc.sync.dma_start(out=w2_raw[e:P:2], in_=w2_rows[e])
         for d, p in enumerate((pos1, pos2, pos3)):
             nc.sync.dma_start(pos_t[d][:], p)
         gate_t = keep.tile([P, D, V], F32, name="gate_t")
@@ -102,10 +103,10 @@ def tile_picked_sub_mlp_silu_sub_e_kernel(tc, xT, w1, w2, gate, offs, pos1, pos2
         w1_scales = keep.tile([P, H], U8, name="w1_scales", align_bytes=64)
 
         def cast_w1(raw, m_base, engine_copy, m0, m1, t0, t1):
-            src = raw[:].rearrange("p j (m t) -> p m j t", t=PACK)
+            src = raw[:].rearrange("p j (a t e) -> p a t j e", t=PACK, e=2)
             engine_copy(
-                out=w1g[:].rearrange("p t m j -> p m j t")[:, m_base + m0 : m_base + m1, :, t0:t1],
-                in_=src[:, m0:m1, :, t0:t1],
+                out=w1g[:].rearrange("p t (a e) j -> p a t j e", e=2)[:, m0 // 2 : m1 // 2, t0:t1],
+                in_=src[:, m0 // 2 : m1 // 2, t0:t1],
             )
 
         def quant_w1(t):
@@ -124,9 +125,11 @@ def tile_picked_sub_mlp_silu_sub_e_kernel(tc, xT, w1, w2, gate, offs, pos1, pos2
         quant_x(xg_lo, 0, 0, P)
         xg_1 = keep.tile([P, P, PACK], BF16, name="xg_1", align_bytes=64)
         weave_x(nc.scalar.copy, U32, xg_1[:], 0, P)
-        for t0, m_vec in ((0, 86), (2, 80)):
-            cast_w1(w1_b, 0, nc.vector.tensor_copy, 0, m_vec, t0, t0 + 2)
-            cast_w1(w1_b, 0, nc.scalar.copy, m_vec, P, t0, t0 + 2)
+        cast_w1(w1_b, 0, nc.vector.tensor_copy, 0, 80, 0, 2)
+        cast_w1(w1_b, 0, nc.scalar.copy, 80, P, 0, 2)
+        cast_w1(w1_b, 0, nc.vector.tensor_copy, 0, 72, 2, 4)
+        for t in (2, 3):
+            cast_w1(w1_b, 0, nc.scalar.copy, 72, P, t, t + 1)
         for t in range(PACK):
             quant_w1(t)
         xg_hi = [shared.tile([P, P, PACK], BF16, name=f"xg_hi{c}", align_bytes=64, offset=(c + 1) * 1024) for c in range(2)]
@@ -145,7 +148,7 @@ def tile_picked_sub_mlp_silu_sub_e_kernel(tc, xT, w1, w2, gate, offs, pos1, pos2
         nc.vector.tensor_copy(out=w2g_v, in_=w2_v)
 
         CUTS = [(0, 128), (128, 256), (256, 384), (384, 448), (448, 512)]
-        h_codes = keep.tile([P, S], U32, name="h_codes", align_bytes=64)
+        h_codes = shared.tile([P, S], U32, name="h_codes", align_bytes=64, offset=8192)
         h_scales = keep.tile([P, S], U8, name="h_scales", align_bytes=64)
         hg = [keep.tile([P, b - a, PACK], BF16, name=f"hg{a}", align_bytes=64) for a, b in CUTS]
         y_t = [keep.tile([P, S], F32, name=f"y_t{h}") for h in range(2)]

@@ -35,14 +35,11 @@ def tile_picked_sub_mlp_silu_sub_e_kernel(tc, xT, w1, w2, gate, offs, pos1, pos2
         w1_rows = w1.rearrange("(p j) c -> p j c", j=PACK)
         w2_rows = w2.rearrange("(a j e) n -> e a j n", j=PACK, e=2)
 
-        X1_CUT = 512
         x_raw0 = keep.tile([P, 2, T], F32, name="x_raw0")
         nc.sync.dma_start(out=x_raw0[:], in_=x_rows[:, 0:2, :])
         nc.sync.dma_start(offs_t[:], offs)
-        x_raw1a = keep.tile([P, 2, X1_CUT], F32, name="x_raw1a")
-        nc.sync.dma_start(out=x_raw1a[:], in_=x_rows[:, 2:4, 0:X1_CUT])
-        x_raw1b = keep.tile([P, 2, T - X1_CUT], F32, name="x_raw1b")
-        nc.sync.dma_start(out=x_raw1b[:], in_=x_rows[:, 2:4, X1_CUT:T])
+        x_raw1 = keep.tile([P, 2, T], F32, name="x_raw1")
+        nc.sync.dma_start(out=x_raw1[:], in_=x_rows[:, 2:4, :])
         w1_b = shared.tile([P, PACK, H], F32, name="w1_b", align_bytes=64, offset=0)
         nc.sync.dma_start(out=w1_b[:], in_=w1_rows)
         w2_raw = shared.tile([P, PACK, N], F32, name="w2_raw", align_bytes=64, offset=8192)
@@ -78,12 +75,13 @@ def tile_picked_sub_mlp_silu_sub_e_kernel(tc, xT, w1, w2, gate, offs, pos1, pos2
 
         def gather_x(u):
             window = x_pair[u][:].rearrange("p t e -> p (t e)").bitcast(U32)
-            nc.vector.tensor_copy(out=first_words[:, :, u], in_=window.indirect(offs_t[:, 0 : P // 16]))
             if u == 0:
+                nc.vector.tensor_copy(out=first_words[:, :, u], in_=window.indirect(offs_t[:, 0 : P // 16]))
                 nc.vector.tensor_copy(out=picked[:, u, :], in_=window.indirect(offs_t[:, P // 16 : S // 16]))
             else:
                 nc.vector.tensor_copy(out=picked[:, u, 0:P], in_=window.indirect(offs_t[:, P // 16 : 2 * P // 16]))
-                nc.vector.tensor_copy(out=picked[:, u, P:], in_=window.indirect(offs_t[:, 2 * P // 16 : S // 16]))
+                nc.vector.tensor_copy(out=first_words[:, :, u], in_=window.indirect(offs_t[:, 0 : P // 16]))
+                nc.vector.tensor_copy(out=picked[:, u, P : 2 * P], in_=window.indirect(offs_t[:, 2 * P // 16 : 3 * P // 16]))
 
         def weave_x(engine_copy, word, dst, a, b):
             engine_copy(
@@ -119,8 +117,7 @@ def tile_picked_sub_mlp_silu_sub_e_kernel(tc, xT, w1, w2, gate, offs, pos1, pos2
 
         cast_x(0, x_raw0[:], 0, T, 688)
         gather_x(0)
-        cast_x(1, x_raw1a[:], 0, X1_CUT, 0)
-        cast_x(1, x_raw1b[:], X1_CUT, T - X1_CUT, 336)
+        cast_x(1, x_raw1[:], 0, T, 688)
         gather_x(1)
         quant_x(xg_lo, 0, 0, P)
         xg_1 = keep.tile([P, P, PACK], BF16, name="xg_1", align_bytes=64)
@@ -135,17 +132,21 @@ def tile_picked_sub_mlp_silu_sub_e_kernel(tc, xT, w1, w2, gate, offs, pos1, pos2
         xg_hi = [shared.tile([P, P, PACK], BF16, name=f"xg_hi{c}", align_bytes=64, offset=(c + 1) * 1024) for c in range(2)]
         x_codes[1] = shared.tile([P, P], U32, name="x_codes1", align_bytes=64, offset=3072)
         quant_x(xg_1, P, P, 2 * P)
-        for c in range(2):
-            weave_x(nc.scalar.copy, U32, xg_hi[c][:], (c + 1) * P, (c + 2) * P)
-        for c in range(2):
-            quant_x(xg_hi[c], (c + 2) * P, (c + 2) * P, (c + 3) * P)
+        weave_x(nc.scalar.copy, U32, xg_hi[0][:], P, 2 * P)
+        quant_x(xg_hi[0], 2 * P, 2 * P, 3 * P)
+        last_words = xg_hi[1][:].rearrange("p s t -> p (s t)").bitcast(U32).rearrange("p (s u) -> p s u", u=2)
+        nc.scalar.copy(out=last_words[:, :, 0], in_=picked[:, 0, 2 * P : 3 * P])
+        window1 = x_pair[1][:].rearrange("p t e -> p (t e)").bitcast(U32)
+        nc.vector.tensor_copy(out=last_words[:, :, 1], in_=window1.indirect(offs_t[:, 3 * P // 16 : S // 16]))
+        quant_x(xg_hi[1], 3 * P, 3 * P, 4 * P)
 
         w2g = shared.tile([P, N, PACK], BF16, name="w2g", align_bytes=64, offset=0)
         w2_codes = keep.tile([P, N], U32, name="w2_codes", align_bytes=64)
         w2_scales = keep.tile([P, N], U8, name="w2_scales", align_bytes=64)
         w2g_v = w2g[:].rearrange("p (c i) j -> p c j i", i=4)
         w2_v = w2_raw[:].rearrange("p j (c i) -> p c j i", i=4)
-        nc.vector.tensor_copy(out=w2g_v, in_=w2_v)
+        for q in range(2):
+            nc.vector.tensor_copy(out=w2g_v[:, q * 32 : (q + 1) * 32], in_=w2_v[:, q * 32 : (q + 1) * 32])
 
         CUTS = [(0, 128), (128, 256), (256, 384), (384, 448), (448, 512)]
         h_codes = shared.tile([P, S], U32, name="h_codes", align_bytes=64, offset=8192)

@@ -59,29 +59,20 @@ def tile_picked_sub_mlp_silu_sub_e_kernel(tc, xT, w1, w2, gate, offs, pos1, pos2
 
         x_pair = [keep.tile([P, T, 2], BF16, name=f"x_pair{u}") for u in range(2)]
 
-        def cast_x(u, raw, t0, n, n_vec):
+        def cast_x(engine_copy, u, raw, a, b):
             src = raw.rearrange("p e (c i) -> p c e i", i=4)
-            dst = x_pair[u][:, t0 : t0 + n, :].rearrange("p (c i) e -> p c e i", i=4)
-            cut = n_vec // 4
-            if cut:
-                nc.vector.tensor_copy(out=dst[:, :cut], in_=src[:, :cut])
-            nc.scalar.copy(out=dst[:, cut:], in_=src[:, cut:])
+            dst = x_pair[u][:].rearrange("p (c i) e -> p c e i", i=4)
+            engine_copy(out=dst[:, a // 4 : b // 4], in_=src[:, a // 4 : b // 4])
 
-        picked = keep.tile([P, 2, S - P], U32, name="picked")
+        picked = keep.tile([P, 2, 2 * P], U32, name="picked")
         xg_lo = keep.tile([P, P, PACK], BF16, name="xg_lo", align_bytes=64)
         first_words = xg_lo[:].rearrange("p s t -> p (s t)").bitcast(U32).rearrange("p (s u) -> p s u", u=2)
         x_codes = {c: keep.tile([P, P], U32, name=f"x_codes{c}", align_bytes=64) for c in (0, 2, 3)}
         x_scales = keep.tile([P, S], U8, name="x_scales", align_bytes=64)
 
-        def gather_x(u):
+        def gather_x(dst, u, a, b):
             window = x_pair[u][:].rearrange("p t e -> p (t e)").bitcast(U32)
-            if u == 0:
-                nc.vector.tensor_copy(out=first_words[:, :, u], in_=window.indirect(offs_t[:, 0 : P // 16]))
-                nc.vector.tensor_copy(out=picked[:, u, :], in_=window.indirect(offs_t[:, P // 16 : S // 16]))
-            else:
-                nc.vector.tensor_copy(out=picked[:, u, 0:P], in_=window.indirect(offs_t[:, P // 16 : 2 * P // 16]))
-                nc.vector.tensor_copy(out=first_words[:, :, u], in_=window.indirect(offs_t[:, 0 : P // 16]))
-                nc.vector.tensor_copy(out=picked[:, u, P : 2 * P], in_=window.indirect(offs_t[:, 2 * P // 16 : 3 * P // 16]))
+            nc.vector.tensor_copy(out=dst, in_=window.indirect(offs_t[:, a // 16 : b // 16]))
 
         def weave_x(engine_copy, word, dst, a, b):
             engine_copy(
@@ -115,19 +106,26 @@ def tile_picked_sub_mlp_silu_sub_e_kernel(tc, xT, w1, w2, gate, offs, pos1, pos2
                 in_=w1g[:, t, :, :].rearrange("p m j -> p (m j)"),
             )
 
-        cast_x(0, x_raw0[:], 0, T, 688)
-        gather_x(0)
-        cast_x(1, x_raw1[:], 0, T, 688)
-        gather_x(1)
+        cast_x(nc.vector.tensor_copy, 0, x_raw0[:], 0, 688)
+        cast_x(nc.scalar.copy, 0, x_raw0[:], 688, T)
+        gather_x(first_words[:, :, 0], 0, 0, P)
+        gather_x(picked[:, 0, :], 0, P, 3 * P)
+        cast_x(nc.vector.tensor_copy, 1, x_raw1[:], 0, 328)
+        cast_x(nc.vector.tensor_copy, 1, x_raw1[:], 328, 656)
+        cast_x(nc.scalar.copy, 1, x_raw1[:], 656, T)
+        last_pair0 = x_raw1[:, 0, 0:P].bitcast(U32)
+        gather_x(last_pair0, 0, 3 * P, S)
+        gather_x(picked[:, 1, 0:P], 1, P, 2 * P)
+        gather_x(first_words[:, :, 1], 1, 0, P)
+        gather_x(picked[:, 1, P : 2 * P], 1, 2 * P, 3 * P)
         quant_x(xg_lo, 0, 0, P)
         xg_1 = keep.tile([P, P, PACK], BF16, name="xg_1", align_bytes=64)
         weave_x(nc.scalar.copy, U32, xg_1[:], 0, P)
-        cast_w1(w1_b, 0, nc.vector.tensor_copy, 0, 80, 0, 2)
-        cast_w1(w1_b, 0, nc.scalar.copy, 80, P, 0, 2)
-        cast_w1(w1_b, 0, nc.vector.tensor_copy, 0, 72, 2, 4)
-        for t in (2, 3):
-            cast_w1(w1_b, 0, nc.scalar.copy, 72, P, t, t + 1)
-        for t in range(PACK):
+        cast_w1(w1_b, 0, nc.vector.tensor_copy, 0, 24, 2, 3)
+        cast_w1(w1_b, 0, nc.vector.tensor_copy, 0, P, 0, 2)
+        cast_w1(w1_b, 0, nc.scalar.copy, 24, P, 2, 3)
+        cast_w1(w1_b, 0, nc.scalar.copy, 0, P, 3, 4)
+        for t in (2, 0, 1, 3):
             quant_w1(t)
         xg_hi = [shared.tile([P, P, PACK], BF16, name=f"xg_hi{c}", align_bytes=64, offset=(c + 1) * 1024) for c in range(2)]
         x_codes[1] = shared.tile([P, P], U32, name="x_codes1", align_bytes=64, offset=3072)
@@ -135,29 +133,39 @@ def tile_picked_sub_mlp_silu_sub_e_kernel(tc, xT, w1, w2, gate, offs, pos1, pos2
         weave_x(nc.scalar.copy, U32, xg_hi[0][:], P, 2 * P)
         quant_x(xg_hi[0], 2 * P, 2 * P, 3 * P)
         last_words = xg_hi[1][:].rearrange("p s t -> p (s t)").bitcast(U32).rearrange("p (s u) -> p s u", u=2)
-        nc.scalar.copy(out=last_words[:, :, 0], in_=picked[:, 0, 2 * P : 3 * P])
-        window1 = x_pair[1][:].rearrange("p t e -> p (t e)").bitcast(U32)
-        nc.vector.tensor_copy(out=last_words[:, :, 1], in_=window1.indirect(offs_t[:, 3 * P // 16 : S // 16]))
+        nc.scalar.copy(out=last_words[:, :, 0], in_=last_pair0)
+        gather_x(last_words[:, :, 1], 1, 3 * P, S)
         quant_x(xg_hi[1], 3 * P, 3 * P, 4 * P)
 
-        w2g = shared.tile([P, N, PACK], BF16, name="w2g", align_bytes=64, offset=0)
-        w2_codes = keep.tile([P, N], U32, name="w2_codes", align_bytes=64)
+        w2_codes = [keep.tile([P, P], U32, name="w2_codes0", align_bytes=64)]
         w2_scales = keep.tile([P, N], U8, name="w2_scales", align_bytes=64)
-        w2g_v = w2g[:].rearrange("p (c i) j -> p c j i", i=4)
         w2_v = w2_raw[:].rearrange("p j (c i) -> p c j i", i=4)
-        for q in range(2):
-            nc.vector.tensor_copy(out=w2g_v[:, q * 32 : (q + 1) * 32], in_=w2_v[:, q * 32 : (q + 1) * 32])
+
+        def cast_w2(h, offset):
+            w2g = shared.tile([P, P, PACK], BF16, name=f"w2g{h}", align_bytes=64, offset=offset)
+            nc.vector.tensor_copy(out=w2g[:].rearrange("p (c i) j -> p c j i", i=4), in_=w2_v[:, h * 32 : (h + 1) * 32])
+            return w2g
+
+        def quant_w2(h, w2g):
+            cols = slice(h * P, (h + 1) * P)
+            nc.vector.quantize_mx(
+                out=w2_codes[h][:].bitcast(FP8X4), scales=w2_scales[:, cols], in_=w2g[:].rearrange("p n j -> p (n j)")
+            )
+
+        w2g_a = cast_w2(0, 1024)
 
         CUTS = [(0, 128), (128, 256), (256, 384), (384, 448), (448, 512)]
-        h_codes = shared.tile([P, S], U32, name="h_codes", align_bytes=64, offset=8192)
+        h_codes = keep.tile([P, S], U32, name="h_codes", align_bytes=64)
         h_scales = keep.tile([P, S], U8, name="h_scales", align_bytes=64)
-        hg = [keep.tile([P, b - a, PACK], BF16, name=f"hg{a}", align_bytes=64) for a, b in CUTS]
+        hg = [
+            shared.tile([P, b - a, PACK], BF16, name=f"hg{a}", align_bytes=64, offset=16384 + 2048 * i) for i, (a, b) in enumerate(CUTS)
+        ]
         y_t = [keep.tile([P, S], F32, name=f"y_t{h}") for h in range(2)]
 
         def layer1(c):
             a, b = c * P, (c + 1) * P
             ps = psum.tile([P, PACK, P], F32, name=f"h_ps{c}", tag=f"bank{c}")
-            for t in (range(PACK) if c == 0 else reversed(range(PACK))):
+            for t in ((2, 0, 1, 3) if c == 0 else reversed(range(PACK))):
                 nc.tensor.matmul_mx(
                     out=ps[:, t, :],
                     lhsT=w1_codes[:, t * P : (t + 1) * P].bitcast(FP8X4),
@@ -182,7 +190,7 @@ def tile_picked_sub_mlp_silu_sub_e_kernel(tc, xT, w1, w2, gate, offs, pos1, pos2
         def layer2(dst, h, a, b):
             nc.tensor.matmul_mx(
                 out=dst,
-                lhsT=w2_codes[:, h * P : (h + 1) * P].bitcast(FP8X4),
+                lhsT=w2_codes[h][:].bitcast(FP8X4),
                 lhsT_scale=w2_scales[:, h * P : (h + 1) * P],
                 rhs=h_codes[:, a:b].bitcast(FP8X4),
                 rhs_scale=h_scales[:, a:b],
@@ -197,9 +205,8 @@ def tile_picked_sub_mlp_silu_sub_e_kernel(tc, xT, w1, w2, gate, offs, pos1, pos2
         ya_last = [psum.tile([P, 64], F32, name=f"ya_last{q}", tag=f"bank{6 + q}") for q in range(2)]
         yb = psum.tile([P, S], F32, name="yb", tag="bank5")
         quant_h(0)
-        nc.vector.quantize_mx(
-            out=w2_codes[:].bitcast(FP8X4), scales=w2_scales[:], in_=w2g[:].rearrange("p n j -> p (n j)")
-        )
+        quant_w2(0, w2g_a)
+        w2g_b = cast_w2(1, 16384)
         quant_h(1)
         layer2(ya_main[:], 0, 0, 256)
         quant_h(2)
@@ -208,6 +215,8 @@ def tile_picked_sub_mlp_silu_sub_e_kernel(tc, xT, w1, w2, gate, offs, pos1, pos2
         layer2(ya_last[0][:], 0, 384, 448)
         quant_h(4)
         layer2(ya_last[1][:], 0, 448, 512)
+        w2_codes.append(shared.tile([P, P], U32, name="w2_codes1", align_bytes=64, offset=16384 + 2048 * 4))
+        quant_w2(1, w2g_b)
         layer2(yb[:], 1, 0, S)
         nc.scalar.copy(out=y_t[0][:, 0:256], in_=ya_main[:])
         nc.scalar.copy(out=y_t[0][:, 256:384], in_=ya_mid[:])

@@ -52,7 +52,7 @@ def tile_picked_sub_mlp_silu_sub_e_kernel(tc, xT, w1, w2, gate, offs, pos1, pos2
 
         warm = keep.tile([P, 1], F32, name="warm")
         warm_o = keep.tile([P, 1], F32, name="warm_o")
-        nc.vector.memset(warm[:], 0.0)
+        nc.gpsimd.memset(warm[:], 0.0)
         nc.scalar.activation(warm_o[:], warm[:], SILU)
         ident = keep.tile([P, P], F32, name="ident")
         make_identity(nc, ident[:])

@@ -1,19 +1,18 @@
 from contextlib import ExitStack
 
 import concourse.mybir as mybir
-from concourse.masks import make_identity
 
 K, T, D, S, V, H, N = 512, 1024, 3, 512, 256, 512, 256
 FLOPS = 2 * S * (K * H + H * N) + 2 * D * N * V
 
 F32 = mybir.dt.float32
 BF16 = mybir.dt.bfloat16
-I32 = mybir.dt.int32
 U32 = mybir.dt.uint32
 U16 = mybir.dt.uint16
 U8 = mybir.dt.uint8
 FP8X4 = mybir.dt.float8_e4m3fn_x4
 SILU = mybir.ActivationFunctionType.Silu
+COPY = mybir.ActivationFunctionType.Copy
 MULT = mybir.AluOpType.mult
 ADD = mybir.AluOpType.add
 
@@ -25,234 +24,164 @@ def tile_picked_sub_mlp_silu_sub_e_kernel(tc, xT, w1, w2, gate, offs, pos1, pos2
     nc = tc.nc
     with ExitStack() as ctx:
         keep = ctx.enter_context(tc.tile_pool(name="keep", bufs=1))
-        shared = ctx.enter_context(tc.tile_pool(name="shared", bufs=1))
         psum = ctx.enter_context(tc.psum_pool(name="psum", bufs=1))
 
         offs_t = keep.tile([P, S // 16], U16, name="offs_t")
         pos_t = [keep.tile([P, V // 16], U16, name=f"pos_t{d}") for d in range(D)]
 
-        x_rows = xT.rearrange("(p j) t -> p j t", j=PACK)
-        w1_rows = w1.rearrange("(p j) c -> p j c", j=PACK)
-        w2_rows = w2.rearrange("(a j e) n -> e a j n", j=PACK, e=2)
-
-        x_raw0 = keep.tile([P, 2, T], F32, name="x_raw0")
-        nc.sync.dma_start(out=x_raw0[:], in_=x_rows[:, 0:2, :])
+        w1_raw = keep.tile([P, PACK, H], F32, name="w1_raw")
+        nc.sync.dma_start(out=w1_raw[:], in_=w1.rearrange("(p j) c -> p j c", j=PACK))
         nc.sync.dma_start(offs_t[:], offs)
-        x_raw1 = keep.tile([P, 2, T], F32, name="x_raw1")
-        nc.sync.dma_start(out=x_raw1[:], in_=x_rows[:, 2:4, :])
-        w1_b = shared.tile([P, PACK, H], F32, name="w1_b", align_bytes=64, offset=0)
-        nc.sync.dma_start(out=w1_b[:], in_=w1_rows)
-        w2_raw = shared.tile([P, PACK, N], F32, name="w2_raw", align_bytes=64, offset=8192)
-        for e in range(2):
-            nc.sync.dma_start(out=w2_raw[e:P:2], in_=w2_rows[e])
-        for d, p in enumerate((pos1, pos2, pos3)):
-            nc.sync.dma_start(pos_t[d][:], p)
+        x_rows = xT.rearrange("(p j) t -> p j t", j=PACK)
+        x_plane = [keep.tile([P, T], F32, name=f"x_plane{j}") for j in range(PACK)]
+        for j in range(PACK):
+            nc.sync.dma_start(out=x_plane[j][:], in_=x_rows[:, j, :])
+        w2_raw = keep.tile([P, PACK, N], F32, name="w2_raw")
+        nc.sync.dma_start(out=w2_raw[:], in_=w2.rearrange("(p j) n -> p j n", j=PACK))
         gate_t = keep.tile([P, D, V], F32, name="gate_t")
         nc.sync.dma_start(out=gate_t[:], in_=gate[:, 0:P, :].rearrange("d p v -> p d v"))
+        for d, p in enumerate((pos1, pos2, pos3)):
+            nc.sync.dma_start(pos_t[d][:], p)
 
         warm = keep.tile([P, 1], F32, name="warm")
         warm_o = keep.tile([P, 1], F32, name="warm_o")
         nc.gpsimd.memset(warm[:], 0.0)
         nc.scalar.activation(warm_o[:], warm[:], SILU)
-        ident = keep.tile([P, P], F32, name="ident")
-        make_identity(nc, ident[:])
 
-        x_pair = [keep.tile([P, T, 2], BF16, name=f"x_pair{u}") for u in range(2)]
+        def quant(codes, scales, src):
+            nc.vector.quantize_mx(out=codes.bitcast(FP8X4), scales=scales, in_=src)
 
-        def cast_x(engine_copy, u, raw, a, b):
-            src = raw.rearrange("p e (c i) -> p c e i", i=4)
-            dst = x_pair[u][:].rearrange("p (c i) e -> p c e i", i=4)
-            engine_copy(out=dst[:, a // 4 : b // 4], in_=src[:, a // 4 : b // 4])
-
-        picked = keep.tile([P, 2, 2 * P], U32, name="picked")
-        xg_lo = keep.tile([P, P, PACK], BF16, name="xg_lo", align_bytes=64)
-        first_words = xg_lo[:].rearrange("p s t -> p (s t)").bitcast(U32).rearrange("p (s u) -> p s u", u=2)
-        x_codes = {c: keep.tile([P, P], U32, name=f"x_codes{c}", align_bytes=64) for c in (0, 2, 3)}
-        x_scales = keep.tile([P, S], U8, name="x_scales", align_bytes=64)
-
-        def gather_x(dst, u, a, b):
-            window = x_pair[u][:].rearrange("p t e -> p (t e)").bitcast(U32)
-            nc.vector.tensor_copy(out=dst, in_=window.indirect(offs_t[:, a // 16 : b // 16]))
-
-        def weave_x(engine_copy, word, dst, a, b):
-            engine_copy(
-                out=dst.rearrange("p s t -> p (s t)").bitcast(word).rearrange("p (c i u) -> p c u i", u=2, i=2),
-                in_=picked[:, :, a:b].bitcast(word).rearrange("p u (c i) -> p c u i", i=2),
-            )
-
-        def quant_x(src, s0, a, b):
-            nc.vector.quantize_mx(
-                out=x_codes[a // P][:].bitcast(FP8X4),
-                scales=x_scales[:, a:b],
-                in_=src[:, a - s0 : b - s0, :].rearrange("p s t -> p (s t)"),
-            )
-
-        w1g = keep.tile([P, PACK, P, PACK], BF16, name="w1g", align_bytes=64)
+        w1g = keep.tile([P, PACK * H], BF16, name="w1g", align_bytes=64)
         w1_codes = keep.tile([P, H], U32, name="w1_codes", align_bytes=64)
         w1_scales = keep.tile([P, H], U8, name="w1_scales", align_bytes=64)
+        w1_src = w1_raw[:].rearrange("p j (m t) -> p m j t", t=PACK)
+        w1_dst = w1g[:].rearrange("p (t m j) -> p m j t", t=PACK, j=PACK)
+        W1_VEC = 88
+        for a in range(0, W1_VEC, W1_VEC // 4):
+            nc.vector.tensor_copy(out=w1_dst[:, a : a + W1_VEC // 4], in_=w1_src[:, a : a + W1_VEC // 4])
+        nc.scalar.copy(out=w1_dst[:, W1_VEC:P], in_=w1_src[:, W1_VEC:P])
+        for t in range(PACK):
+            quant(w1_codes[:, t * P : (t + 1) * P], w1_scales[:, t * P : (t + 1) * P], w1g[:, t * H : (t + 1) * H])
 
-        def cast_w1(raw, m_base, engine_copy, m0, m1, t0, t1):
-            src = raw[:].rearrange("p j (a t e) -> p a t j e", t=PACK, e=2)
+        def picked(j, a, b):
+            return x_plane[j][:].indirect(offs_t[:, a // 16 : b // 16])
+
+        xg_lo = keep.tile([P, 2 * P * PACK], BF16, name="xg_lo", align_bytes=64)
+        lo_slots = xg_lo[:].rearrange("p (s t) -> p s t", t=PACK)
+        planes_all = keep.tile([P, PACK, 2 * P], BF16, name="planes_all")
+        planes_hi = [planes_all[:, :, c * P : (c + 1) * P] for c in range(2)]
+        last_1 = keep.tile([P, P], BF16, name="last_1")
+        xg_hi = [keep.tile([P, P * PACK], BF16, name=f"xg_hi{c}", align_bytes=64) for c in range(2)]
+        x_codes = [keep.tile([P, P], U32, name=f"x_codes{c}", align_bytes=64) for c in range(4)]
+        x_scales = [keep.tile([P, P], U8, name=f"x_scales{c}", align_bytes=64) for c in range(4)]
+
+        for j in range(PACK - 1):
+            for a in (0, P):
+                nc.vector.tensor_copy(out=lo_slots[:, a : a + P, j], in_=picked(j, a, a + P))
+            nc.scalar.activation(planes_all[:, j, :], picked(j, 2 * P, S), COPY)
+        nc.vector.tensor_copy(out=lo_slots[:, 0:P, 3], in_=picked(3, 0, P))
+        nc.scalar.activation(last_1[:], picked(3, P, 2 * P), COPY)
+        for c in range(2):
+            nc.scalar.activation(planes_hi[c][:, 3, :], picked(3, (2 + c) * P, (3 + c) * P), COPY)
+        nc.vector.tensor_copy(out=lo_slots[:, P : 2 * P, 3], in_=last_1[:])
+
+        def weave(engine_copy, c):
             engine_copy(
-                out=w1g[:].rearrange("p t (a e) j -> p a t j e", e=2)[:, m0 // 2 : m1 // 2, t0:t1],
-                in_=src[:, m0 // 2 : m1 // 2, t0:t1],
+                out=xg_hi[c][:].rearrange("p (s i t) -> p s t i", i=4, t=PACK),
+                in_=planes_hi[c].rearrange("p t (s i) -> p s t i", i=4),
             )
 
-        def quant_w1(t):
-            cols = slice(t * P, (t + 1) * P)
-            nc.vector.quantize_mx(
-                out=w1_codes[:, cols].bitcast(FP8X4),
-                scales=w1_scales[:, cols],
-                in_=w1g[:, t, :, :].rearrange("p m j -> p (m j)"),
-            )
-
-        cast_x(nc.vector.tensor_copy, 0, x_raw0[:], 0, 688)
-        cast_x(nc.scalar.copy, 0, x_raw0[:], 688, T)
-        gather_x(first_words[:, :, 0], 0, 0, P)
-        gather_x(picked[:, 0, :], 0, P, 3 * P)
-        cast_x(nc.vector.tensor_copy, 1, x_raw1[:], 0, 328)
-        cast_x(nc.vector.tensor_copy, 1, x_raw1[:], 328, 656)
-        cast_x(nc.scalar.copy, 1, x_raw1[:], 656, T)
-        last_pair0 = x_raw1[:, 0, 0:P].bitcast(U32)
-        gather_x(last_pair0, 0, 3 * P, S)
-        gather_x(picked[:, 1, 0:P], 1, P, 2 * P)
-        gather_x(first_words[:, :, 1], 1, 0, P)
-        gather_x(picked[:, 1, P : 2 * P], 1, 2 * P, 3 * P)
-        quant_x(xg_lo, 0, 0, P)
-        xg_1 = keep.tile([P, P, PACK], BF16, name="xg_1", align_bytes=64)
-        weave_x(nc.scalar.copy, U32, xg_1[:], 0, P)
-        cast_w1(w1_b, 0, nc.vector.tensor_copy, 0, 24, 2, 3)
-        cast_w1(w1_b, 0, nc.vector.tensor_copy, 0, P, 0, 2)
-        cast_w1(w1_b, 0, nc.scalar.copy, 24, P, 2, 3)
-        cast_w1(w1_b, 0, nc.scalar.copy, 0, P, 3, 4)
-        for t in (2, 0, 1, 3):
-            quant_w1(t)
-        xg_hi = [shared.tile([P, P, PACK], BF16, name=f"xg_hi{c}", align_bytes=64, offset=(c + 1) * 1024) for c in range(2)]
-        x_codes[1] = shared.tile([P, P], U32, name="x_codes1", align_bytes=64, offset=3072)
-        quant_x(xg_1, P, P, 2 * P)
-        weave_x(nc.scalar.copy, U32, xg_hi[0][:], P, 2 * P)
-        quant_x(xg_hi[0], 2 * P, 2 * P, 3 * P)
-        last_words = xg_hi[1][:].rearrange("p s t -> p (s t)").bitcast(U32).rearrange("p (s u) -> p s u", u=2)
-        nc.scalar.copy(out=last_words[:, :, 0], in_=last_pair0)
-        gather_x(last_words[:, :, 1], 1, 3 * P, S)
-        quant_x(xg_hi[1], 3 * P, 3 * P, 4 * P)
-
-        w2_codes = [keep.tile([P, P], U32, name="w2_codes0", align_bytes=64)]
+        w2g = keep.tile([P, N * PACK], BF16, name="w2g", align_bytes=64)
+        w2_codes = keep.tile([P, N], U32, name="w2_codes", align_bytes=64)
         w2_scales = keep.tile([P, N], U8, name="w2_scales", align_bytes=64)
-        w2_v = w2_raw[:].rearrange("p j (c i) -> p c j i", i=4)
+        w2_src = w2_raw[:].rearrange("p j (c i) -> p c j i", i=4)
+        w2_dst = w2g[:].rearrange("p (c i j) -> p c j i", i=4, j=PACK)
 
-        def cast_w2(h, offset):
-            w2g = shared.tile([P, P, PACK], BF16, name=f"w2g{h}", align_bytes=64, offset=offset)
-            nc.vector.tensor_copy(out=w2g[:].rearrange("p (c i) j -> p c j i", i=4), in_=w2_v[:, h * 32 : (h + 1) * 32])
-            return w2g
-
-        def quant_w2(h, w2g):
-            cols = slice(h * P, (h + 1) * P)
-            nc.vector.quantize_mx(
-                out=w2_codes[h][:].bitcast(FP8X4), scales=w2_scales[:, cols], in_=w2g[:].rearrange("p n j -> p (n j)")
-            )
-
-        w2g_a = cast_w2(0, 1024)
+        quant(x_codes[0][:], x_scales[0][:], xg_lo[:, 0 : P * PACK])
+        quant(x_codes[1][:], x_scales[1][:], xg_lo[:, P * PACK : 2 * P * PACK])
+        weave(nc.vector.tensor_copy, 0)
+        weave(nc.vector.tensor_copy, 1)
+        quant(x_codes[2][:], x_scales[2][:], xg_hi[0][:])
+        quant(x_codes[3][:], x_scales[3][:], xg_hi[1][:])
+        nc.vector.tensor_copy(out=w2_dst, in_=w2_src)
 
         CUTS = [(0, 128), (128, 256), (256, 384), (384, 448), (448, 512)]
         h_codes = keep.tile([P, S], U32, name="h_codes", align_bytes=64)
         h_scales = keep.tile([P, S], U8, name="h_scales", align_bytes=64)
-        hg = [
-            shared.tile([P, b - a, PACK], BF16, name=f"hg{a}", align_bytes=64, offset=16384 + 2048 * i) for i, (a, b) in enumerate(CUTS)
-        ]
+        hg = [keep.tile([P, b - a, PACK], BF16, name=f"hg{a}", align_bytes=64) for a, b in CUTS]
         y_t = [keep.tile([P, S], F32, name=f"y_t{h}") for h in range(2)]
 
-        def layer1(c):
-            a, b = c * P, (c + 1) * P
-            ps = psum.tile([P, PACK, P], F32, name=f"h_ps{c}", tag=f"bank{c}")
-            for t in ((2, 0, 1, 3) if c == 0 else reversed(range(PACK))):
-                nc.tensor.matmul_mx(
-                    out=ps[:, t, :],
-                    lhsT=w1_codes[:, t * P : (t + 1) * P].bitcast(FP8X4),
-                    lhsT_scale=w1_scales[:, t * P : (t + 1) * P],
-                    rhs=x_codes[c][:].bitcast(FP8X4),
-                    rhs_scale=x_scales[:, a:b],
-                    start=True,
-                    stop=True,
-                )
-            for i, (s0, s1) in enumerate(CUTS):
-                if a <= s0 < b:
-                    nc.scalar.activation(hg[i][:], ps[:, :, s0 - a : s1 - a].rearrange("p t s -> p s t"), SILU)
-
-        def quant_h(c):
-            a, b = CUTS[c]
-            nc.vector.quantize_mx(
-                out=h_codes[:, a:b].bitcast(FP8X4),
-                scales=h_scales[:, a:b],
-                in_=hg[c][:].rearrange("p s t -> p (s t)"),
-            )
-
-        def layer2(dst, h, a, b):
+        def mx(dst, w_codes, w_scales, m_codes, m_scales):
             nc.tensor.matmul_mx(
                 out=dst,
-                lhsT=w2_codes[h][:].bitcast(FP8X4),
-                lhsT_scale=w2_scales[:, h * P : (h + 1) * P],
-                rhs=h_codes[:, a:b].bitcast(FP8X4),
-                rhs_scale=h_scales[:, a:b],
+                lhsT=w_codes.bitcast(FP8X4),
+                lhsT_scale=w_scales,
+                rhs=m_codes.bitcast(FP8X4),
+                rhs_scale=m_scales,
                 start=True,
                 stop=True,
             )
 
         for c in range(4):
-            layer1(c)
-        ya_main = psum.tile([P, 256], F32, name="ya_main", tag="bank4")
-        ya_mid = psum.tile([P, P], F32, name="ya_mid", tag="bank0")
-        ya_last = [psum.tile([P, 64], F32, name=f"ya_last{q}", tag=f"bank{6 + q}") for q in range(2)]
-        yb = psum.tile([P, S], F32, name="yb", tag="bank5")
+            ps = psum.tile([P, PACK, P], F32, name=f"h_ps{c}", tag=f"bank{c}")
+            for t in range(PACK):
+                cols = slice(t * P, (t + 1) * P)
+                mx(ps[:, t, :], w1_codes[:, cols], w1_scales[:, cols], x_codes[c][:], x_scales[c][:])
+            for i, (s0, s1) in enumerate(CUTS):
+                if c * P <= s0 < (c + 1) * P:
+                    nc.scalar.activation(hg[i][:], ps[:, :, s0 - c * P : s1 - c * P].rearrange("p t s -> p s t"), SILU)
+
+        def quant_h(i):
+            a, b = CUTS[i]
+            quant(h_codes[:, a:b], h_scales[:, a:b], hg[i][:].rearrange("p s t -> p (s t)"))
+
+        PIECES = [(0, 256), (256, 384), (384, 448), (448, 512)]
+        SPANS = [[(0, 256, 4), (256, 448, 0), (448, 512, 6)], [(0, 384, 5), (384, 512, 7)]]
+        y_ps = [{a: psum.tile([P, b - a], F32, name=f"y_ps{h}{a}", tag=f"bank{bank}") for a, b, bank in SPANS[h]} for h in range(2)]
+
+        def layer2(i):
+            a, b = PIECES[i]
+            for h in range(2):
+                cols = slice(h * P, (h + 1) * P)
+                start = max(s for s in y_ps[h] if s <= a)
+                mx(y_ps[h][start][:, a - start : b - start], w2_codes[:, cols], w2_scales[:, cols], h_codes[:, a:b], h_scales[:, a:b])
+
         quant_h(0)
-        quant_w2(0, w2g_a)
-        w2g_b = cast_w2(1, 16384)
+        quant(w2_codes[:], w2_scales[:], w2g[:])
         quant_h(1)
-        layer2(ya_main[:], 0, 0, 256)
-        quant_h(2)
-        layer2(ya_mid[:], 0, 256, 384)
-        quant_h(3)
-        layer2(ya_last[0][:], 0, 384, 448)
-        quant_h(4)
-        layer2(ya_last[1][:], 0, 448, 512)
-        w2_codes.append(shared.tile([P, P], U32, name="w2_codes1", align_bytes=64, offset=16384 + 2048 * 4))
-        quant_w2(1, w2g_b)
-        layer2(yb[:], 1, 0, S)
-        nc.scalar.copy(out=y_t[0][:, 0:256], in_=ya_main[:])
-        nc.scalar.copy(out=y_t[0][:, 256:384], in_=ya_mid[:])
-        nc.scalar.copy(out=y_t[0][:, 384:448], in_=ya_last[0][:])
-        nc.scalar.copy(out=y_t[0][:, 448:512], in_=ya_last[1][:])
-        nc.scalar.copy(out=y_t[1][:], in_=yb[:])
+        layer2(0)
+        for i in range(1, 4):
+            quant_h(i + 1)
+            layer2(i)
+        for h, engine_copy in enumerate((nc.scalar.copy, nc.vector.tensor_copy)):
+            for a, b, bank in SPANS[h]:
+                engine_copy(out=y_t[h][:, a:b], in_=y_ps[h][a][:])
 
-        def fetch(dst, h, d, a, b):
-            nc.vector.tensor_tensor(dst, y_t[h][:].indirect(pos_t[d][:, a // 16 : b // 16]), gate_t[:, d, a:b], MULT)
+        def near(h, d, a, b):
+            return y_t[h][:].indirect(pos_t[d][:, a // 16 : b // 16])
 
-        prod_a = [keep.tile([P, V], F32, name=f"prod_a{d}") for d in range(D)]
-        prod_b = [keep.tile([P, V], F32, name=f"prod_b{d}") for d in range(D)]
-        sum_t = [psum.tile([P, P], F32, name=f"sum_t{q}", tag=f"bank{1 + q}") for q in range(2)]
-        for d in range(D):
-            fetch(prod_a[d][:], 0, d, 0, V)
-            for q in range(2):
-                nc.tensor.matmul(
-                    sum_t[q][:], prod_a[d][:, q * P : (q + 1) * P], ident[:], start=(d == 0), stop=(d == D - 1), is_transpose=True
-                )
-        sum_sb = [keep.tile([P, P], F32, name=f"sum_sb{q}") for q in range(2)]
-        back = psum.tile([P, V], F32, name="back", tag="bank3")
-        for q in range(2):
-            nc.scalar.copy(out=sum_sb[q][:], in_=sum_t[q][:])
-            nc.tensor.transpose(back[:, q * P : (q + 1) * P], sum_sb[q][:], ident[:])
-        res_a = keep.tile([P, V], F32, name="res_a")
-        nc.scalar.copy(out=res_a[:], in_=back[:])
-        nc.scalar.dma_start(out=out[0:P, :], in_=res_a[:])
+        prod = [[keep.tile([P, V], F32, name=f"prod{h}{d}") for d in range(D)] for h in range(2)]
+        plain = {hd: keep.tile([P, V], F32, name=f"plain{hd[0]}{hd[1]}") for hd in ((0, 1), (1, 0), (1, 1), (0, 2))}
+        part = [keep.tile([P, V], F32, name=f"part{h}") for h in range(2)]
+        res = [keep.tile([P, V], F32, name=f"res{h}") for h in range(2)]
+        for (h, d), tile in plain.items():
+            nc.scalar.activation(tile[:], near(h, d, 0, V), COPY)
 
-        fetch(prod_b[0][:], 1, 0, 0, V)
-        fetch(prod_b[1][:], 1, 1, 0, V)
-        LAST = 192
-        fetch(prod_b[2][:, 0:LAST], 1, 2, 0, LAST)
-        part = keep.tile([P, V], F32, name="part")
-        nc.vector.tensor_tensor(part[:], prod_b[0][:], prod_b[1][:], ADD)
-        fetch(prod_b[2][:, LAST:V], 1, 2, LAST, V)
-        for q, cols in enumerate((slice(0, LAST), slice(LAST, V))):
-            res_b = keep.tile([P, cols.stop - cols.start], F32, name=f"res_b{q}")
-            nc.vector.tensor_tensor(res_b[:], part[:, cols], prod_b[2][:, cols], ADD)
-            nc.sync.dma_start(out=out[P : 2 * P, cols], in_=res_b[:])
+        def weigh(h, d):
+            src = plain[h, d][:] if (h, d) in plain else near(h, d, 0, V)
+            nc.vector.tensor_tensor(prod[h][d][:], src, gate_t[:, d, :], MULT)
+
+        def finish(h, d):
+            nc.vector.tensor_tensor(res[h][:], part[h][:], prod[h][d][:], ADD)
+            nc.sync.dma_start(out=out[h * P : (h + 1) * P, :], in_=res[h][:])
+
+        weigh(0, 0)
+        weigh(1, 2)
+        weigh(0, 1)
+        weigh(1, 0)
+        nc.vector.tensor_tensor(part[0][:], prod[0][0][:], prod[0][1][:], ADD)
+        weigh(1, 1)
+        nc.vector.tensor_tensor(part[1][:], prod[1][2][:], prod[1][0][:], ADD)
+        weigh(0, 2)
+        finish(1, 1)
+        finish(0, 2)

@@ -24,6 +24,7 @@ def tile_picked_sub_mlp_silu_sub_e_kernel(tc, xT, w1, w2, gate, offs, pos1, pos2
     nc = tc.nc
     with ExitStack() as ctx:
         keep = ctx.enter_context(tc.tile_pool(name="keep", bufs=1))
+        shared = ctx.enter_context(tc.tile_pool(name="shared", bufs=1))
         psum = ctx.enter_context(tc.psum_pool(name="psum", bufs=1))
 
         offs_t = keep.tile([P, S // 16], U16, name="offs_t")
@@ -33,9 +34,12 @@ def tile_picked_sub_mlp_silu_sub_e_kernel(tc, xT, w1, w2, gate, offs, pos1, pos2
         nc.sync.dma_start(out=w1_raw[:], in_=w1.rearrange("(p j) c -> p j c", j=PACK))
         nc.sync.dma_start(offs_t[:], offs)
         x_rows = xT.rearrange("(p j) t -> p j t", j=PACK)
-        x_plane = [keep.tile([P, T], F32, name=f"x_plane{j}") for j in range(PACK)]
-        for j in range(PACK):
-            nc.sync.dma_start(out=x_plane[j][:], in_=x_rows[:, j, :])
+        x_first = keep.tile([P, 2, T], F32, name="x_first")
+        nc.sync.dma_start(out=x_first[:], in_=x_rows[:, 0:2, :])
+        x_late = [keep.tile([P, T], F32, name=f"x_late{j}") for j in range(2)]
+        for j in range(2):
+            nc.sync.dma_start(out=x_late[j][:], in_=x_rows[:, 2 + j, :])
+        x_plane = [x_first[:, 0, :], x_first[:, 1, :], x_late[0][:], x_late[1][:]]
         w2_raw = keep.tile([P, PACK, N], F32, name="w2_raw")
         nc.sync.dma_start(out=w2_raw[:], in_=w2.rearrange("(p j) n -> p j n", j=PACK))
         gate_t = keep.tile([P, D, V], F32, name="gate_t")
@@ -64,20 +68,24 @@ def tile_picked_sub_mlp_silu_sub_e_kernel(tc, xT, w1, w2, gate, offs, pos1, pos2
             quant(w1_codes[:, t * P : (t + 1) * P], w1_scales[:, t * P : (t + 1) * P], w1g[:, t * H : (t + 1) * H])
 
         def picked(j, a, b):
-            return x_plane[j][:].indirect(offs_t[:, a // 16 : b // 16])
+            return x_plane[j].indirect(offs_t[:, a // 16 : b // 16])
 
         xg_lo = keep.tile([P, 2 * P * PACK], BF16, name="xg_lo", align_bytes=64)
         lo_slots = xg_lo[:].rearrange("p (s t) -> p s t", t=PACK)
-        planes_all = keep.tile([P, PACK, 2 * P], BF16, name="planes_all")
+        planes_all = shared.tile([P, PACK, 2 * P], F32, name="planes_all", align_bytes=64, offset=0)
         planes_hi = [planes_all[:, :, c * P : (c + 1) * P] for c in range(2)]
         last_1 = keep.tile([P, P], BF16, name="last_1")
         xg_hi = [keep.tile([P, P * PACK], BF16, name=f"xg_hi{c}", align_bytes=64) for c in range(2)]
         x_codes = [keep.tile([P, P], U32, name=f"x_codes{c}", align_bytes=64) for c in range(4)]
         x_scales = [keep.tile([P, P], U8, name=f"x_scales{c}", align_bytes=64) for c in range(4)]
 
+        first_1 = keep.tile([P, P], F32, name="first_1")
+        nc.scalar.activation(first_1[:], picked(0, P, 2 * P), COPY)
         for j in range(PACK - 1):
-            for a in (0, P):
+            for a in (0, P) if j else (0,):
                 nc.vector.tensor_copy(out=lo_slots[:, a : a + P, j], in_=picked(j, a, a + P))
+            if j == 1:
+                nc.vector.tensor_copy(out=lo_slots[:, P : 2 * P, 0], in_=first_1[:])
             nc.scalar.activation(planes_all[:, j, :], picked(j, 2 * P, S), COPY)
         nc.vector.tensor_copy(out=lo_slots[:, 0:P, 3], in_=picked(3, 0, P))
         nc.scalar.activation(last_1[:], picked(3, P, 2 * P), COPY)
@@ -91,7 +99,7 @@ def tile_picked_sub_mlp_silu_sub_e_kernel(tc, xT, w1, w2, gate, offs, pos1, pos2
                 in_=planes_hi[c].rearrange("p t (s i) -> p s t i", i=4),
             )
 
-        w2g = keep.tile([P, N * PACK], BF16, name="w2g", align_bytes=64)
+        w2g = shared.tile([P, N * PACK], BF16, name="w2g", align_bytes=64, offset=0)
         w2_codes = keep.tile([P, N], U32, name="w2_codes", align_bytes=64)
         w2_scales = keep.tile([P, N], U8, name="w2_scales", align_bytes=64)
         w2_src = w2_raw[:].rearrange("p j (c i) -> p c j i", i=4)

@@ -61,11 +61,9 @@ def tile_picked_sub_mlp_silu_sub_e_kernel(tc, xT, w1, w2, gate, offs, pos1, pos2
         w1_src = w1_raw[:].rearrange("p j (m t) -> p m j t", t=PACK)
         w1_dst = w1g[:].rearrange("p (t m j) -> p m j t", t=PACK, j=PACK)
         W1_VEC = 88
-        for a in range(0, W1_VEC, W1_VEC // 4):
-            nc.vector.tensor_copy(out=w1_dst[:, a : a + W1_VEC // 4], in_=w1_src[:, a : a + W1_VEC // 4])
+        nc.vector.tensor_copy(out=w1_dst[:, 0:W1_VEC], in_=w1_src[:, 0:W1_VEC])
         nc.scalar.copy(out=w1_dst[:, W1_VEC:P], in_=w1_src[:, W1_VEC:P])
-        for t in range(PACK):
-            quant(w1_codes[:, t * P : (t + 1) * P], w1_scales[:, t * P : (t + 1) * P], w1g[:, t * H : (t + 1) * H])
+        quant(w1_codes[:], w1_scales[:], w1g[:])
 
         def picked(j, a, b):
             return x_plane[j].indirect(offs_t[:, a // 16 : b // 16])
@@ -82,8 +80,8 @@ def tile_picked_sub_mlp_silu_sub_e_kernel(tc, xT, w1, w2, gate, offs, pos1, pos2
         first_1 = keep.tile([P, P], F32, name="first_1")
         nc.scalar.activation(first_1[:], picked(0, P, 2 * P), COPY)
         for j in range(PACK - 1):
-            for a in (0, P) if j else (0,):
-                nc.vector.tensor_copy(out=lo_slots[:, a : a + P, j], in_=picked(j, a, a + P))
+            width = 2 * P if j else P
+            nc.vector.tensor_copy(out=lo_slots[:, 0:width, j], in_=picked(j, 0, width))
             if j == 1:
                 nc.vector.tensor_copy(out=lo_slots[:, P : 2 * P, 0], in_=first_1[:])
             nc.scalar.activation(planes_all[:, j, :], picked(j, 2 * P, S), COPY)

@@ -167,27 +167,30 @@ def tile_picked_sub_mlp_silu_sub_e_kernel(tc, xT, w1, w2, gate, offs, pos1, pos2
             return y_t[h][:].indirect(pos_t[d][:, a // 16 : b // 16])
 
         prod = [[keep.tile([P, V], F32, name=f"prod{h}{d}") for d in range(D)] for h in range(2)]
-        plain = {hd: keep.tile([P, V], F32, name=f"plain{hd[0]}{hd[1]}") for hd in ((0, 1), (1, 0), (1, 1), (0, 2))}
+        plain = {hd: keep.tile([P, V], F32, name=f"plain{hd[0]}{hd[1]}") for hd in ((0, 1), (0, 2), (1, 0), (1, 1))}
         part = [keep.tile([P, V], F32, name=f"part{h}") for h in range(2)]
-        res = [keep.tile([P, V], F32, name=f"res{h}") for h in range(2)]
         for (h, d), tile in plain.items():
             nc.scalar.activation(tile[:], near(h, d, 0, V), COPY)
 
-        def weigh(h, d):
-            src = plain[h, d][:] if (h, d) in plain else near(h, d, 0, V)
-            nc.vector.tensor_tensor(prod[h][d][:], src, gate_t[:, d, :], MULT)
+        def weigh(h, d, a=0, b=V):
+            src = plain[h, d][:, a:b] if (h, d) in plain else near(h, d, a, b)
+            nc.vector.tensor_tensor(prod[h][d][:, a:b], src, gate_t[:, d, a:b], MULT)
 
-        def finish(h, d):
-            nc.vector.tensor_tensor(res[h][:], part[h][:], prod[h][d][:], ADD)
-            nc.sync.dma_start(out=out[h * P : (h + 1) * P, :], in_=res[h][:])
+        def finish(h, d, a, b):
+            res = keep.tile([P, b - a], F32, name=f"res{h}{a}")
+            nc.vector.tensor_tensor(res[:], part[h][:, a:b], prod[h][d][:, a:b], ADD)
+            nc.sync.dma_start(out=out[h * P : (h + 1) * P, a:b], in_=res[:])
 
+        LAST = 128
         weigh(0, 0)
         weigh(1, 2)
         weigh(0, 1)
-        weigh(1, 0)
-        nc.vector.tensor_tensor(part[0][:], prod[0][0][:], prod[0][1][:], ADD)
-        weigh(1, 1)
-        nc.vector.tensor_tensor(part[1][:], prod[1][2][:], prod[1][0][:], ADD)
         weigh(0, 2)
-        finish(1, 1)
-        finish(0, 2)
+        nc.vector.tensor_tensor(part[0][:], prod[0][0][:], prod[0][1][:], ADD)
+        weigh(1, 0)
+        finish(0, 2, 0, V)
+        nc.vector.tensor_tensor(part[1][:], prod[1][2][:], prod[1][0][:], ADD)
+        weigh(1, 1, 0, LAST)
+        weigh(1, 1, LAST, V)
+        finish(1, 1, 0, LAST)
+        finish(1, 1, LAST, V)

@@ -176,10 +176,11 @@ def tile_picked_sub_mlp_silu_sub_e_kernel(tc, xT, w1, w2, gate, offs, pos1, pos2
             src = plain[h, d][:, a:b] if (h, d) in plain else near(h, d, a, b)
             nc.vector.tensor_tensor(prod[h][d][:, a:b], src, gate_t[:, d, a:b], MULT)
 
-        def finish(h, d, a, b):
-            res = keep.tile([P, b - a], F32, name=f"res{h}{a}")
-            nc.vector.tensor_tensor(res[:], part[h][:, a:b], prod[h][d][:, a:b], ADD)
-            nc.sync.dma_start(out=out[h * P : (h + 1) * P, a:b], in_=res[:])
+        def finish(h, d, cuts):
+            res = keep.tile([P, V], F32, name=f"res{h}")
+            for a, b in cuts:
+                nc.vector.tensor_tensor(res[:, a:b], part[h][:, a:b], prod[h][d][:, a:b], ADD)
+            nc.sync.dma_start(out=out[h * P : (h + 1) * P, :], in_=res[:])
 
         LAST = 128
         weigh(0, 0)
@@ -188,9 +189,8 @@ def tile_picked_sub_mlp_silu_sub_e_kernel(tc, xT, w1, w2, gate, offs, pos1, pos2
         weigh(0, 2)
         nc.vector.tensor_tensor(part[0][:], prod[0][0][:], prod[0][1][:], ADD)
         weigh(1, 0)
-        finish(0, 2, 0, V)
+        finish(0, 2, [(0, V)])
         nc.vector.tensor_tensor(part[1][:], prod[1][2][:], prod[1][0][:], ADD)
         weigh(1, 1, 0, LAST)
         weigh(1, 1, LAST, V)
-        finish(1, 1, 0, LAST)
-        finish(1, 1, LAST, V)
+        finish(1, 1, [(0, LAST), (LAST, V)])

@@ -30,12 +30,12 @@ def tile_picked_sub_mlp_silu_sub_e_kernel(tc, xT, w1, w2, gate, offs, pos1, pos2
         offs_t = keep.tile([P, S // 16], U16, name="offs_t")
         pos_t = [keep.tile([P, V // 16], U16, name=f"pos_t{d}") for d in range(D)]
 
-        w1_raw = keep.tile([P, PACK, H], F32, name="w1_raw")
-        nc.sync.dma_start(out=w1_raw[:], in_=w1.rearrange("(p j) c -> p j c", j=PACK))
-        nc.sync.dma_start(offs_t[:], offs)
         x_rows = xT.rearrange("(p j) t -> p j t", j=PACK)
         x_first = keep.tile([P, 2, T], F32, name="x_first")
         nc.sync.dma_start(out=x_first[:], in_=x_rows[:, 0:2, :])
+        nc.sync.dma_start(offs_t[:], offs)
+        w1_raw = keep.tile([P, PACK, H], F32, name="w1_raw")
+        nc.sync.dma_start(out=w1_raw[:], in_=w1.rearrange("(p j) c -> p j c", j=PACK))
         x_late = [keep.tile([P, T], F32, name=f"x_late{j}") for j in range(2)]
         for j in range(2):
             nc.sync.dma_start(out=x_late[j][:], in_=x_rows[:, 2 + j, :])
@@ -61,9 +61,6 @@ def tile_picked_sub_mlp_silu_sub_e_kernel(tc, xT, w1, w2, gate, offs, pos1, pos2
         w1_src = w1_raw[:].rearrange("p j (m t) -> p m j t", t=PACK)
         w1_dst = w1g[:].rearrange("p (t m j) -> p m j t", t=PACK, j=PACK)
         W1_VEC = 88
-        nc.vector.tensor_copy(out=w1_dst[:, 0:W1_VEC], in_=w1_src[:, 0:W1_VEC])
-        nc.scalar.copy(out=w1_dst[:, W1_VEC:P], in_=w1_src[:, W1_VEC:P])
-        quant(w1_codes[:], w1_scales[:], w1g[:])
 
         def picked(j, a, b):
             return x_plane[j].indirect(offs_t[:, a // 16 : b // 16])
@@ -72,24 +69,24 @@ def tile_picked_sub_mlp_silu_sub_e_kernel(tc, xT, w1, w2, gate, offs, pos1, pos2
         lo_slots = xg_lo[:].rearrange("p (s t) -> p s t", t=PACK)
         planes_all = shared.tile([P, PACK, 2 * P], F32, name="planes_all", align_bytes=64, offset=0)
         planes_hi = [planes_all[:, :, c * P : (c + 1) * P] for c in range(2)]
-        last_1 = keep.tile([P, P], BF16, name="last_1")
+        late_1 = keep.tile([P, 2, P], BF16, name="late_1")
         xg_hi = [keep.tile([P, P * PACK], BF16, name=f"xg_hi{c}", align_bytes=64) for c in range(2)]
         x_codes = [keep.tile([P, P], U32, name=f"x_codes{c}", align_bytes=64) for c in range(4)]
         x_scales = [keep.tile([P, P], U8, name=f"x_scales{c}", align_bytes=64) for c in range(4)]
 
-        first_1 = keep.tile([P, P], F32, name="first_1")
-        nc.scalar.activation(first_1[:], picked(0, P, 2 * P), COPY)
-        for j in range(PACK - 1):
-            width = 2 * P if j else P
-            nc.vector.tensor_copy(out=lo_slots[:, 0:width, j], in_=picked(j, 0, width))
-            if j == 1:
-                nc.vector.tensor_copy(out=lo_slots[:, P : 2 * P, 0], in_=first_1[:])
+        for j in range(2):
+            nc.vector.tensor_copy(out=lo_slots[:, :, j], in_=picked(j, 0, 2 * P))
             nc.scalar.activation(planes_all[:, j, :], picked(j, 2 * P, S), COPY)
-        nc.vector.tensor_copy(out=lo_slots[:, 0:P, 3], in_=picked(3, 0, P))
-        nc.scalar.activation(last_1[:], picked(3, P, 2 * P), COPY)
-        for c in range(2):
-            nc.scalar.activation(planes_hi[c][:, 3, :], picked(3, (2 + c) * P, (3 + c) * P), COPY)
-        nc.vector.tensor_copy(out=lo_slots[:, P : 2 * P, 3], in_=last_1[:])
+        nc.vector.tensor_copy(out=w1_dst[:, 0:W1_VEC], in_=w1_src[:, 0:W1_VEC])
+        nc.scalar.copy(out=w1_dst[:, W1_VEC:P], in_=w1_src[:, W1_VEC:P])
+        quant(w1_codes[:], w1_scales[:], w1g[:])
+        for j in range(2, PACK):
+            nc.vector.tensor_copy(out=lo_slots[:, 0:P, j], in_=picked(j, 0, P))
+            nc.scalar.activation(late_1[:, j - 2, :], picked(j, P, 2 * P), COPY)
+            step = P if j == PACK - 1 else 2 * P
+            for a in range(0, 2 * P, step):
+                nc.scalar.activation(planes_all[:, j, a : a + step], picked(j, 2 * P + a, 2 * P + a + step), COPY)
+        nc.vector.tensor_copy(out=lo_slots[:, P : 2 * P, 2:4], in_=late_1[:].rearrange("p t s -> p s t"))
 
         def weave(engine_copy, c):
             engine_copy(

@@ -18,103 +18,50 @@ ADD = mybir.AluOpType.add
 
 P = 128
 PACK = 4
+CHUNKS = S // P
+X_LO_BYTES = 2 * P * PACK * 2
+W1_VECTOR = 88
+SILU_CUTS = [(0, 128), (128, 256), (256, 384), (384, 448), (448, 512)]
+Y_PASSES = [[(0, 256), (256, 384), (384, 448), (448, 512)], [(0, 256), (256, 384), (384, 512)]]
+Y_COPIES = [[(0, 256, 4), (256, 448, 0), (448, 512, 6)], [(0, 384, 5), (384, 512, 7)]]
+SCALAR_FETCHES = [(0, 1), (0, 2), (1, 0), (1, 1)]
 
 
 def tile_picked_sub_mlp_silu_sub_e_kernel(tc, xT, w1, w2, gate, offs, pos1, pos2, pos3, out):
     nc = tc.nc
     with ExitStack() as ctx:
         keep = ctx.enter_context(tc.tile_pool(name="keep", bufs=1))
-        shared = ctx.enter_context(tc.tile_pool(name="shared", bufs=1))
+        turns = ctx.enter_context(tc.tile_pool(name="turns", bufs=1))
         psum = ctx.enter_context(tc.psum_pool(name="psum", bufs=1))
 
         offs_t = keep.tile([P, S // 16], U16, name="offs_t")
         pos_t = [keep.tile([P, V // 16], U16, name=f"pos_t{d}") for d in range(D)]
-
         x_rows = xT.rearrange("(p j) t -> p j t", j=PACK)
         x_first = keep.tile([P, 2, T], F32, name="x_first")
         nc.sync.dma_start(out=x_first[:], in_=x_rows[:, 0:2, :])
         nc.sync.dma_start(offs_t[:], offs)
         w1_raw = keep.tile([P, PACK, H], F32, name="w1_raw")
         nc.sync.dma_start(out=w1_raw[:], in_=w1.rearrange("(p j) c -> p j c", j=PACK))
-        x_late = [keep.tile([P, T], F32, name=f"x_late{j}") for j in range(2)]
+        x_last = [keep.tile([P, T], F32, name=f"x_last{j}") for j in range(2)]
         for j in range(2):
-            nc.sync.dma_start(out=x_late[j][:], in_=x_rows[:, 2 + j, :])
-        x_plane = [x_first[:, 0, :], x_first[:, 1, :], x_late[0][:], x_late[1][:]]
+            nc.sync.dma_start(out=x_last[j][:], in_=x_rows[:, 2 + j, :])
+        planes = [x_first[:, 0, :], x_first[:, 1, :], x_last[0][:], x_last[1][:]]
         w2_raw = keep.tile([P, PACK, N], F32, name="w2_raw")
         nc.sync.dma_start(out=w2_raw[:], in_=w2.rearrange("(p j) n -> p j n", j=PACK))
         gate_t = keep.tile([P, D, V], F32, name="gate_t")
         nc.sync.dma_start(out=gate_t[:], in_=gate[:, 0:P, :].rearrange("d p v -> p d v"))
-        for d, p in enumerate((pos1, pos2, pos3)):
-            nc.sync.dma_start(pos_t[d][:], p)
+        for d, pos in enumerate((pos1, pos2, pos3)):
+            nc.sync.dma_start(pos_t[d][:], pos)
 
-        warm = keep.tile([P, 1], F32, name="warm")
-        warm_o = keep.tile([P, 1], F32, name="warm_o")
-        nc.gpsimd.memset(warm[:], 0.0)
-        nc.scalar.activation(warm_o[:], warm[:], SILU)
+        preload_in = keep.tile([P, 1], F32, name="preload_in")
+        preload_out = keep.tile([P, 1], F32, name="preload_out")
+        nc.gpsimd.memset(preload_in[:], 0.0)
+        nc.scalar.activation(preload_out[:], preload_in[:], SILU)
 
-        def quant(codes, scales, src):
-            nc.vector.quantize_mx(out=codes.bitcast(FP8X4), scales=scales, in_=src)
+        def quantise(codes, scales, values):
+            nc.vector.quantize_mx(out=codes.bitcast(FP8X4), scales=scales, in_=values)
 
-        w1g = keep.tile([P, PACK * H], BF16, name="w1g", align_bytes=64)
-        w1_codes = keep.tile([P, H], U32, name="w1_codes", align_bytes=64)
-        w1_scales = keep.tile([P, H], U8, name="w1_scales", align_bytes=64)
-        w1_src = w1_raw[:].rearrange("p j (m t) -> p m j t", t=PACK)
-        w1_dst = w1g[:].rearrange("p (t m j) -> p m j t", t=PACK, j=PACK)
-        W1_VEC = 88
-
-        def picked(j, a, b):
-            return x_plane[j].indirect(offs_t[:, a // 16 : b // 16])
-
-        xg_lo = keep.tile([P, 2 * P * PACK], BF16, name="xg_lo", align_bytes=64)
-        lo_slots = xg_lo[:].rearrange("p (s t) -> p s t", t=PACK)
-        planes_all = shared.tile([P, PACK, 2 * P], F32, name="planes_all", align_bytes=64, offset=0)
-        planes_hi = [planes_all[:, :, c * P : (c + 1) * P] for c in range(2)]
-        late_1 = keep.tile([P, 2, P], BF16, name="late_1")
-        xg_hi = [keep.tile([P, P * PACK], BF16, name=f"xg_hi{c}", align_bytes=64) for c in range(2)]
-        x_codes = [keep.tile([P, P], U32, name=f"x_codes{c}", align_bytes=64) for c in range(4)]
-        x_scales = [keep.tile([P, P], U8, name=f"x_scales{c}", align_bytes=64) for c in range(4)]
-
-        for j in range(2):
-            nc.vector.tensor_copy(out=lo_slots[:, :, j], in_=picked(j, 0, 2 * P))
-            nc.scalar.activation(planes_all[:, j, :], picked(j, 2 * P, S), COPY)
-        nc.vector.tensor_copy(out=w1_dst[:, 0:W1_VEC], in_=w1_src[:, 0:W1_VEC])
-        nc.scalar.copy(out=w1_dst[:, W1_VEC:P], in_=w1_src[:, W1_VEC:P])
-        quant(w1_codes[:], w1_scales[:], w1g[:])
-        for j in range(2, PACK):
-            nc.vector.tensor_copy(out=lo_slots[:, 0:P, j], in_=picked(j, 0, P))
-            nc.scalar.activation(late_1[:, j - 2, :], picked(j, P, 2 * P), COPY)
-            step = P if j == PACK - 1 else 2 * P
-            for a in range(0, 2 * P, step):
-                nc.scalar.activation(planes_all[:, j, a : a + step], picked(j, 2 * P + a, 2 * P + a + step), COPY)
-        nc.vector.tensor_copy(out=lo_slots[:, P : 2 * P, 2:4], in_=late_1[:].rearrange("p t s -> p s t"))
-
-        def weave(engine_copy, c):
-            engine_copy(
-                out=xg_hi[c][:].rearrange("p (s i t) -> p s t i", i=4, t=PACK),
-                in_=planes_hi[c].rearrange("p t (s i) -> p s t i", i=4),
-            )
-
-        w2g = shared.tile([P, N * PACK], BF16, name="w2g", align_bytes=64, offset=0)
-        w2_codes = keep.tile([P, N], U32, name="w2_codes", align_bytes=64)
-        w2_scales = keep.tile([P, N], U8, name="w2_scales", align_bytes=64)
-        w2_src = w2_raw[:].rearrange("p j (c i) -> p c j i", i=4)
-        w2_dst = w2g[:].rearrange("p (c i j) -> p c j i", i=4, j=PACK)
-
-        quant(x_codes[0][:], x_scales[0][:], xg_lo[:, 0 : P * PACK])
-        quant(x_codes[1][:], x_scales[1][:], xg_lo[:, P * PACK : 2 * P * PACK])
-        weave(nc.vector.tensor_copy, 0)
-        weave(nc.vector.tensor_copy, 1)
-        quant(x_codes[2][:], x_scales[2][:], xg_hi[0][:])
-        quant(x_codes[3][:], x_scales[3][:], xg_hi[1][:])
-        nc.vector.tensor_copy(out=w2_dst, in_=w2_src)
-
-        CUTS = [(0, 128), (128, 256), (256, 384), (384, 448), (448, 512)]
-        h_codes = keep.tile([P, S], U32, name="h_codes", align_bytes=64)
-        h_scales = keep.tile([P, S], U8, name="h_scales", align_bytes=64)
-        hg = [keep.tile([P, b - a, PACK], BF16, name=f"hg{a}", align_bytes=64) for a, b in CUTS]
-        y_t = [keep.tile([P, S], F32, name=f"y_t{h}") for h in range(2)]
-
-        def mx(dst, w_codes, w_scales, m_codes, m_scales):
+        def multiply(dst, w_codes, w_scales, m_codes, m_scales):
             nc.tensor.matmul_mx(
                 out=dst,
                 lhsT=w_codes.bitcast(FP8X4),
@@ -125,69 +72,119 @@ def tile_picked_sub_mlp_silu_sub_e_kernel(tc, xT, w1, w2, gate, offs, pos1, pos2
                 stop=True,
             )
 
-        for c in range(4):
-            ps = psum.tile([P, PACK, P], F32, name=f"h_ps{c}", tag=f"bank{c}")
+        def picked(j, a, b):
+            return planes[j].indirect(offs_t[:, a // 16 : b // 16])
+
+        x_lo = turns.tile([P, 2 * P * PACK], BF16, name="x_lo", align_bytes=64, offset=0)
+        lo_slots = x_lo[:].rearrange("p (s j) -> p s j", j=PACK)
+        x_2 = keep.tile([P, P, PACK], BF16, name="x_2", align_bytes=64)
+        stage_1 = keep.tile([P, 2, P], BF16, name="stage_1")
+        stage_2a = keep.tile([P, 2, P], F32, name="stage_2a")
+        stage_2b = turns.tile([P, 2, P], BF16, name="stage_2b", align_bytes=64, offset=X_LO_BYTES)
+        stage_3 = keep.tile([P, PACK, P], F32, name="stage_3")
+        x_codes = [keep.tile([P, P], U32, name=f"x_codes{c}", align_bytes=64) for c in range(CHUNKS)]
+        x_scales = [keep.tile([P, P], U8, name=f"x_scales{c}", align_bytes=64) for c in range(CHUNKS)]
+
+        for j in range(2):
+            nc.vector.tensor_copy(out=lo_slots[:, :, j], in_=picked(j, 0, 2 * P))
+            nc.scalar.activation(stage_2a[:, j, :], picked(j, 2 * P, 3 * P), COPY)
+            nc.scalar.activation(stage_3[:, j, :], picked(j, 3 * P, S), COPY)
+        nc.vector.tensor_copy(out=x_2[:, :, 0:2], in_=stage_2a[:].rearrange("p j s -> p s j"))
+
+        w1_bf = keep.tile([P, PACK * H], BF16, name="w1_bf", align_bytes=64)
+        w1_codes = keep.tile([P, H], U32, name="w1_codes", align_bytes=64)
+        w1_scales = keep.tile([P, H], U8, name="w1_scales", align_bytes=64)
+        w1_src = w1_raw[:].rearrange("p j (m t) -> p m j t", t=PACK)
+        w1_dst = w1_bf[:].rearrange("p (t m j) -> p m j t", t=PACK, j=PACK)
+        nc.vector.tensor_copy(out=w1_dst[:, 0:W1_VECTOR], in_=w1_src[:, 0:W1_VECTOR])
+        nc.scalar.copy(out=w1_dst[:, W1_VECTOR:P], in_=w1_src[:, W1_VECTOR:P])
+        quantise(w1_codes[:], w1_scales[:], w1_bf[:])
+
+        for j in range(2, PACK):
+            nc.vector.tensor_copy(out=lo_slots[:, 0:P, j], in_=picked(j, 0, P))
+            nc.scalar.activation(stage_1[:, j - 2, :], picked(j, P, 2 * P), COPY)
+            nc.scalar.activation(stage_2b[:, j - 2, :], picked(j, 2 * P, 3 * P), COPY)
+            nc.scalar.activation(stage_3[:, j, :], picked(j, 3 * P, S), COPY)
+        nc.vector.tensor_copy(out=lo_slots[:, P : 2 * P, 2:PACK], in_=stage_1[:].rearrange("p j s -> p s j"))
+        quantise(x_codes[0][:], x_scales[0][:], x_lo[:, 0 : P * PACK])
+        nc.vector.tensor_copy(out=x_2[:, :, 2:PACK], in_=stage_2b[:].rearrange("p j s -> p s j"))
+        quantise(x_codes[1][:], x_scales[1][:], x_lo[:, P * PACK : 2 * P * PACK])
+        quantise(x_codes[2][:], x_scales[2][:], x_2[:].rearrange("p s j -> p (s j)"))
+        x_3 = turns.tile([P, P * PACK], BF16, name="x_3", align_bytes=64, offset=0)
+        nc.vector.tensor_copy(
+            out=x_3[:].rearrange("p (s i j) -> p s j i", i=4, j=PACK), in_=stage_3[:].rearrange("p j (s i) -> p s j i", i=4)
+        )
+
+        w2_bf = turns.tile([P, N * PACK], BF16, name="w2_bf", align_bytes=64, offset=X_LO_BYTES)
+        w2_codes = keep.tile([P, N], U32, name="w2_codes", align_bytes=64)
+        w2_scales = keep.tile([P, N], U8, name="w2_scales", align_bytes=64)
+        w2_src = w2_raw[:].rearrange("p j (c i) -> p c j i", i=4)
+        w2_dst = w2_bf[:].rearrange("p (c i j) -> p c j i", i=4, j=PACK)
+        groups = N // 4
+        nc.vector.tensor_copy(out=w2_dst[:, 0 : groups // 2], in_=w2_src[:, 0 : groups // 2])
+        quantise(x_codes[3][:], x_scales[3][:], x_3[:])
+        nc.vector.tensor_copy(out=w2_dst[:, groups // 2 :], in_=w2_src[:, groups // 2 :])
+
+        h_bf = [keep.tile([P, b - a, PACK], BF16, name=f"h_bf{a}", align_bytes=64) for a, b in SILU_CUTS]
+        h_codes = keep.tile([P, S], U32, name="h_codes", align_bytes=64)
+        h_scales = keep.tile([P, S], U8, name="h_scales", align_bytes=64)
+        for c in range(CHUNKS):
+            h_ps = psum.tile([P, PACK, P], F32, name=f"h_ps{c}", tag=f"bank{c}")
             for t in range(PACK):
                 cols = slice(t * P, (t + 1) * P)
-                mx(ps[:, t, :], w1_codes[:, cols], w1_scales[:, cols], x_codes[c][:], x_scales[c][:])
-            for i, (s0, s1) in enumerate(CUTS):
-                if c * P <= s0 < (c + 1) * P:
-                    nc.scalar.activation(hg[i][:], ps[:, :, s0 - c * P : s1 - c * P].rearrange("p t s -> p s t"), SILU)
+                multiply(h_ps[:, t, :], w1_codes[:, cols], w1_scales[:, cols], x_codes[c][:], x_scales[c][:])
+            for cut, (a, b) in enumerate(SILU_CUTS):
+                if a // P == c:
+                    nc.scalar.activation(h_bf[cut][:], h_ps[:, :, a - c * P : b - c * P].rearrange("p t s -> p s t"), SILU)
 
-        def quant_h(i):
-            a, b = CUTS[i]
-            quant(h_codes[:, a:b], h_scales[:, a:b], hg[i][:].rearrange("p s t -> p (s t)"))
+        y_t = [keep.tile([P, S], F32, name=f"y_t{half}") for half in range(2)]
+        y_ps = [
+            {a: psum.tile([P, b - a], F32, name=f"y_ps{half}_{a}", tag=f"bank{bank}") for a, b, bank in Y_COPIES[half]}
+            for half in range(2)
+        ]
+        for cut, (cut_a, cut_b) in enumerate(SILU_CUTS):
+            quantise(h_codes[:, cut_a:cut_b], h_scales[:, cut_a:cut_b], h_bf[cut][:].rearrange("p s t -> p (s t)"))
+            if cut == 0:
+                quantise(w2_codes[:], w2_scales[:], w2_bf[:])
+            for half in range(2):
+                cols = slice(half * P, (half + 1) * P)
+                for a, b in Y_PASSES[half]:
+                    if b == cut_b:
+                        base = max(start for start in y_ps[half] if start <= a)
+                        dst = y_ps[half][base][:, a - base : b - base]
+                        multiply(dst, w2_codes[:, cols], w2_scales[:, cols], h_codes[:, a:b], h_scales[:, a:b])
+        for half, engine_copy in enumerate((nc.scalar.copy, nc.vector.tensor_copy)):
+            for a, b, bank in Y_COPIES[half]:
+                engine_copy(out=y_t[half][:, a:b], in_=y_ps[half][a][:])
 
-        PIECES = [(0, 256), (256, 384), (384, 448), (448, 512)]
-        SPANS = [[(0, 256, 4), (256, 448, 0), (448, 512, 6)], [(0, 384, 5), (384, 512, 7)]]
-        y_ps = [{a: psum.tile([P, b - a], F32, name=f"y_ps{h}{a}", tag=f"bank{bank}") for a, b, bank in SPANS[h]} for h in range(2)]
+        def neighbours(half, d, a, b):
+            return y_t[half][:].indirect(pos_t[d][:, a // 16 : b // 16])
 
-        def layer2(i):
-            a, b = PIECES[i]
-            for h in range(2):
-                cols = slice(h * P, (h + 1) * P)
-                start = max(s for s in y_ps[h] if s <= a)
-                mx(y_ps[h][start][:, a - start : b - start], w2_codes[:, cols], w2_scales[:, cols], h_codes[:, a:b], h_scales[:, a:b])
+        term = [[keep.tile([P, V], F32, name=f"term{half}{d}") for d in range(D)] for half in range(2)]
+        fetched = {pair: keep.tile([P, V], F32, name=f"fetched{pair[0]}{pair[1]}") for pair in SCALAR_FETCHES}
+        partial = [keep.tile([P, V], F32, name=f"partial{half}") for half in range(2)]
+        for half, d in SCALAR_FETCHES:
+            nc.scalar.activation(fetched[half, d][:], neighbours(half, d, 0, V), COPY)
 
-        quant_h(0)
-        quant(w2_codes[:], w2_scales[:], w2g[:])
-        quant_h(1)
-        layer2(0)
-        for i in range(1, 4):
-            quant_h(i + 1)
-            layer2(i)
-        for h, engine_copy in enumerate((nc.scalar.copy, nc.vector.tensor_copy)):
-            for a, b, bank in SPANS[h]:
-                engine_copy(out=y_t[h][:, a:b], in_=y_ps[h][a][:])
+        def weigh(half, d, a=0, b=V):
+            values = fetched[half, d][:, a:b] if (half, d) in fetched else neighbours(half, d, a, b)
+            nc.vector.tensor_tensor(term[half][d][:, a:b], values, gate_t[:, d, a:b], MULT)
 
-        def near(h, d, a, b):
-            return y_t[h][:].indirect(pos_t[d][:, a // 16 : b // 16])
-
-        prod = [[keep.tile([P, V], F32, name=f"prod{h}{d}") for d in range(D)] for h in range(2)]
-        plain = {hd: keep.tile([P, V], F32, name=f"plain{hd[0]}{hd[1]}") for hd in ((0, 1), (0, 2), (1, 0), (1, 1))}
-        part = [keep.tile([P, V], F32, name=f"part{h}") for h in range(2)]
-        for (h, d), tile in plain.items():
-            nc.scalar.activation(tile[:], near(h, d, 0, V), COPY)
-
-        def weigh(h, d, a=0, b=V):
-            src = plain[h, d][:, a:b] if (h, d) in plain else near(h, d, a, b)
-            nc.vector.tensor_tensor(prod[h][d][:, a:b], src, gate_t[:, d, a:b], MULT)
-
-        def finish(h, d, cuts):
-            res = keep.tile([P, V], F32, name=f"res{h}")
+        def finish(half, d, cuts):
+            result = keep.tile([P, V], F32, name=f"result{half}")
             for a, b in cuts:
-                nc.vector.tensor_tensor(res[:, a:b], part[h][:, a:b], prod[h][d][:, a:b], ADD)
-            nc.sync.dma_start(out=out[h * P : (h + 1) * P, :], in_=res[:])
+                nc.vector.tensor_tensor(result[:, a:b], partial[half][:, a:b], term[half][d][:, a:b], ADD)
+            nc.sync.dma_start(out=out[half * P : (half + 1) * P, :], in_=result[:])
 
-        LAST = 128
+        column_halves = [(0, V // 2), (V // 2, V)]
         weigh(0, 0)
         weigh(1, 2)
         weigh(0, 1)
         weigh(0, 2)
-        nc.vector.tensor_tensor(part[0][:], prod[0][0][:], prod[0][1][:], ADD)
+        nc.vector.tensor_tensor(partial[0][:], term[0][0][:], term[0][1][:], ADD)
         weigh(1, 0)
         finish(0, 2, [(0, V)])
-        nc.vector.tensor_tensor(part[1][:], prod[1][2][:], prod[1][0][:], ADD)
-        weigh(1, 1, 0, LAST)
-        weigh(1, 1, LAST, V)
-        finish(1, 1, [(0, LAST), (LAST, V)])
+        nc.vector.tensor_tensor(partial[1][:], term[1][2][:], term[1][0][:], ADD)
+        for a, b in column_halves:
+            weigh(1, 1, a, b)
+        finish(1, 1, column_halves)

@@ -21,6 +21,7 @@ PACK = 4
 CHUNKS = S // P
 X_LO_BYTES = 2 * P * PACK * 2
 W1_VECTOR = 88
+WARM_ROWS = 32
 SILU_CUTS = [(0, 128), (128, 256), (256, 384), (384, 448), (448, 512)]
 Y_PASSES = [[(0, 256), (256, 384), (384, 448), (448, 512)], [(0, 256), (256, 384), (384, 512)]]
 Y_COPIES = [[(0, 256, 4), (256, 448, 0), (448, 512, 6)], [(0, 384, 5), (384, 512, 7)]]
@@ -99,6 +100,9 @@ def tile_picked_sub_mlp_silu_sub_e_kernel(tc, xT, w1, w2, gate, offs, pos1, pos2
         nc.vector.tensor_copy(out=w1_dst[:, 0:W1_VECTOR], in_=w1_src[:, 0:W1_VECTOR])
         nc.scalar.copy(out=w1_dst[:, W1_VECTOR:P], in_=w1_src[:, W1_VECTOR:P])
         quantise(w1_codes[:], w1_scales[:], w1_bf[:])
+        warm_ps = psum.tile([WARM_ROWS, H], F32, name="warm_ps", tag="bank4")
+        for width in (H, H, P):
+            multiply(warm_ps[:, 0:width], w1_codes[:, 0:WARM_ROWS], w1_scales[:, 0:WARM_ROWS], w1_codes[:, 0:width], w1_scales[:, 0:width])
 
         for j in range(2, PACK):
             nc.vector.tensor_copy(out=lo_slots[:, 0:P, j], in_=picked(j, 0, P))

@@ -19,8 +19,7 @@ ADD = mybir.AluOpType.add
 P = 128
 PACK = 4
 CHUNKS = S // P
-X_LO_BYTES = 2 * P * PACK * 2
-W1_VECTOR = 88
+W1_VECTOR = 80
 WARM_ROWS = 32
 SILU_CUTS = [(0, 128), (128, 256), (256, 384), (384, 448), (448, 512)]
 Y_PASSES = [[(0, 256), (256, 384), (384, 448), (448, 512)], [(0, 256), (256, 384), (384, 512)]]
@@ -79,9 +78,7 @@ def tile_picked_sub_mlp_silu_sub_e_kernel(tc, xT, w1, w2, gate, offs, pos1, pos2
         x_lo = turns.tile([P, 2 * P * PACK], BF16, name="x_lo", align_bytes=64, offset=0)
         lo_slots = x_lo[:].rearrange("p (s j) -> p s j", j=PACK)
         x_2 = keep.tile([P, P, PACK], BF16, name="x_2", align_bytes=64)
-        stage_1 = keep.tile([P, 2, P], BF16, name="stage_1")
         stage_2a = keep.tile([P, 2, P], F32, name="stage_2a")
-        stage_2b = turns.tile([P, 2, P], BF16, name="stage_2b", align_bytes=64, offset=X_LO_BYTES)
         stage_3 = keep.tile([P, PACK, P], F32, name="stage_3")
         x_codes = [keep.tile([P, P], U32, name=f"x_codes{c}", align_bytes=64) for c in range(CHUNKS)]
         x_scales = [keep.tile([P, P], U8, name=f"x_scales{c}", align_bytes=64) for c in range(CHUNKS)]
@@ -106,12 +103,10 @@ def tile_picked_sub_mlp_silu_sub_e_kernel(tc, xT, w1, w2, gate, offs, pos1, pos2
 
         for j in range(2, PACK):
             nc.vector.tensor_copy(out=lo_slots[:, 0:P, j], in_=picked(j, 0, P))
-            nc.scalar.activation(stage_1[:, j - 2, :], picked(j, P, 2 * P), COPY)
-            nc.scalar.activation(stage_2b[:, j - 2, :], picked(j, 2 * P, 3 * P), COPY)
+            nc.scalar.activation(lo_slots[:, P : 2 * P, j], picked(j, P, 2 * P), COPY)
+            nc.scalar.activation(x_2[:, :, j], picked(j, 2 * P, 3 * P), COPY)
             nc.scalar.activation(stage_3[:, j, :], picked(j, 3 * P, S), COPY)
-        nc.vector.tensor_copy(out=lo_slots[:, P : 2 * P, 2:PACK], in_=stage_1[:].rearrange("p j s -> p s j"))
         quantise(x_codes[0][:], x_scales[0][:], x_lo[:, 0 : P * PACK])
-        nc.vector.tensor_copy(out=x_2[:, :, 2:PACK], in_=stage_2b[:].rearrange("p j s -> p s j"))
         quantise(x_codes[1][:], x_scales[1][:], x_lo[:, P * PACK : 2 * P * PACK])
         quantise(x_codes[2][:], x_scales[2][:], x_2[:].rearrange("p s j -> p (s j)"))
         x_3 = turns.tile([P, P * PACK], BF16, name="x_3", align_bytes=64, offset=0)
@@ -119,7 +114,7 @@ def tile_picked_sub_mlp_silu_sub_e_kernel(tc, xT, w1, w2, gate, offs, pos1, pos2
             out=x_3[:].rearrange("p (s i j) -> p s j i", i=4, j=PACK), in_=stage_3[:].rearrange("p j (s i) -> p s j i", i=4)
         )
 
-        w2_bf = turns.tile([P, N * PACK], BF16, name="w2_bf", align_bytes=64, offset=X_LO_BYTES)
+        w2_bf = keep.tile([P, N * PACK], BF16, name="w2_bf", align_bytes=64)
         w2_codes = keep.tile([P, N], U32, name="w2_codes", align_bytes=64)
         w2_scales = keep.tile([P, N], U8, name="w2_scales", align_bytes=64)
         w2_src = w2_raw[:].rearrange("p j (c i) -> p c j i", i=4)
@@ -157,8 +152,9 @@ def tile_picked_sub_mlp_silu_sub_e_kernel(tc, xT, w1, w2, gate, offs, pos1, pos2
                         base = max(start for start in y_ps[half] if start <= a)
                         dst = y_ps[half][base][:, a - base : b - base]
                         multiply(dst, w2_codes[:, cols], w2_scales[:, cols], h_codes[:, a:b], h_scales[:, a:b])
-        for half, engine_copy in enumerate((nc.scalar.copy, nc.vector.tensor_copy)):
+        for half in range(2):
             for a, b, bank in Y_COPIES[half]:
+                engine_copy = nc.vector.tensor_copy if half == 1 and b < S else nc.scalar.copy
                 engine_copy(out=y_t[half][:, a:b], in_=y_ps[half][a][:])
 
         def neighbours(half, d, a, b):

@@ -127,7 +127,15 @@ def tile_picked_sub_mlp_silu_sub_e_kernel(tc, xT, w1, w2, gate, offs, pos1, pos2
         h_bf = [keep.tile([P, b - a, PACK], BF16, name=f"h_bf{a}", align_bytes=64) for a, b in SILU_CUTS]
         h_codes = keep.tile([P, S], U32, name="h_codes", align_bytes=64)
         h_scales = keep.tile([P, S], U8, name="h_scales", align_bytes=64)
-        for c in range(CHUNKS):
+        h_pairs = keep.tile([P, 2, P, 2], BF16, name="h_pairs")
+        for u, bank in enumerate((0, 7)):
+            pair_ps = psum.tile([P, 2, P], F32, name=f"pair_ps{u}", tag=f"bank{bank}")
+            for e in range(2):
+                cols = slice((2 * u + e) * P, (2 * u + e + 1) * P)
+                multiply(pair_ps[:, e, :], w1_codes[:, cols], w1_scales[:, cols], x_codes[0][:], x_scales[0][:])
+            nc.scalar.activation(h_pairs[:, u], pair_ps[:].rearrange("p e s -> p s e"), SILU)
+        nc.vector.tensor_copy(out=h_bf[0][:].rearrange("p s (u e) -> p s u e", e=2), in_=h_pairs[:].rearrange("p u s e -> p s u e"))
+        for c in range(1, CHUNKS):
             h_ps = psum.tile([P, PACK, P], F32, name=f"h_ps{c}", tag=f"bank{c}")
             for t in range(PACK):
                 cols = slice(t * P, (t + 1) * P)
@@ -142,9 +150,9 @@ def tile_picked_sub_mlp_silu_sub_e_kernel(tc, xT, w1, w2, gate, offs, pos1, pos2
             for half in range(2)
         ]
         for cut, (cut_a, cut_b) in enumerate(SILU_CUTS):
-            quantise(h_codes[:, cut_a:cut_b], h_scales[:, cut_a:cut_b], h_bf[cut][:].rearrange("p s t -> p (s t)"))
             if cut == 0:
                 quantise(w2_codes[:], w2_scales[:], w2_bf[:])
+            quantise(h_codes[:, cut_a:cut_b], h_scales[:, cut_a:cut_b], h_bf[cut][:].rearrange("p s t -> p (s t)"))
             for half in range(2):
                 cols = slice(half * P, (half + 1) * P)
                 for a, b in Y_PASSES[half]:

@@ -19,7 +19,7 @@ ADD = mybir.AluOpType.add
 P = 128
 PACK = 4
 CHUNKS = S // P
-W1_VECTOR = 80
+W1_VECTOR = 32
 WARM_ROWS = 32
 SILU_CUTS = [(0, 128), (128, 256), (256, 384), (384, 448), (448, 512)]
 Y_PASSES = [[(0, 256), (256, 384), (384, 448), (448, 512)], [(0, 256), (256, 384), (384, 512)]]
@@ -92,13 +92,16 @@ def tile_picked_sub_mlp_silu_sub_e_kernel(tc, xT, w1, w2, gate, offs, pos1, pos2
         w1_bf = keep.tile([P, PACK * H], BF16, name="w1_bf", align_bytes=64)
         w1_codes = keep.tile([P, H], U32, name="w1_codes", align_bytes=64)
         w1_scales = keep.tile([P, H], U8, name="w1_scales", align_bytes=64)
-        w1_src = w1_raw[:].rearrange("p j (m t) -> p m j t", t=PACK)
-        w1_dst = w1_bf[:].rearrange("p (t m j) -> p m j t", t=PACK, j=PACK)
-        nc.vector.tensor_copy(out=w1_dst[:, 0:W1_VECTOR], in_=w1_src[:, 0:W1_VECTOR])
-        nc.scalar.copy(out=w1_dst[:, W1_VECTOR:P], in_=w1_src[:, W1_VECTOR:P])
-        quantise(w1_codes[:], w1_scales[:], w1_bf[:])
+        w1_src = w1_raw[:].rearrange("p j (m u e) -> p u m j e", u=2, e=2)
+        w1_dst = w1_bf[:].rearrange("p (u e m j) -> p u m j e", u=2, e=2, j=PACK)
+        nc.vector.tensor_copy(out=w1_dst[:, 0], in_=w1_src[:, 0])
+        nc.vector.tensor_copy(out=w1_dst[:, 1, 0:W1_VECTOR], in_=w1_src[:, 1, 0:W1_VECTOR])
+        nc.scalar.copy(out=w1_dst[:, 1, W1_VECTOR:P], in_=w1_src[:, 1, W1_VECTOR:P])
+        for u in range(2):
+            cols = slice(u * H // 2, (u + 1) * H // 2)
+            quantise(w1_codes[:, cols], w1_scales[:, cols], w1_bf[:, u * PACK * H // 2 : (u + 1) * PACK * H // 2])
         warm_ps = psum.tile([WARM_ROWS, H], F32, name="warm_ps", tag="bank4")
-        for width in (H, H, P):
+        for width in (P, H, H):
             multiply(warm_ps[:, 0:width], w1_codes[:, 0:WARM_ROWS], w1_scales[:, 0:WARM_ROWS], w1_codes[:, 0:width], w1_scales[:, 0:width])
 
         for j in range(2, PACK):

@@ -19,7 +19,7 @@ ADD = mybir.AluOpType.add
 P = 128
 PACK = 4
 CHUNKS = S // P
-W1_VECTOR = 32
+W1_VECTOR = (96, 56)
 WARM_ROWS = 32
 SILU_CUTS = [(0, 128), (128, 256), (256, 384), (384, 448), (448, 512)]
 Y_PASSES = [[(0, 256), (256, 384), (384, 448), (448, 512)], [(0, 256), (256, 384), (384, 512)]]
@@ -31,7 +31,6 @@ def tile_picked_sub_mlp_silu_sub_e_kernel(tc, xT, w1, w2, gate, offs, pos1, pos2
     nc = tc.nc
     with ExitStack() as ctx:
         keep = ctx.enter_context(tc.tile_pool(name="keep", bufs=1))
-        turns = ctx.enter_context(tc.tile_pool(name="turns", bufs=1))
         psum = ctx.enter_context(tc.psum_pool(name="psum", bufs=1))
 
         offs_t = keep.tile([P, S // 16], U16, name="offs_t")
@@ -75,7 +74,7 @@ def tile_picked_sub_mlp_silu_sub_e_kernel(tc, xT, w1, w2, gate, offs, pos1, pos2
         def picked(j, a, b):
             return planes[j].indirect(offs_t[:, a // 16 : b // 16])
 
-        x_lo = turns.tile([P, 2 * P * PACK], BF16, name="x_lo", align_bytes=64, offset=0)
+        x_lo = keep.tile([P, 2 * P * PACK], BF16, name="x_lo", align_bytes=64)
         lo_slots = x_lo[:].rearrange("p (s j) -> p s j", j=PACK)
         x_2 = keep.tile([P, P, PACK], BF16, name="x_2", align_bytes=64)
         stage_2a = keep.tile([P, 2, P], F32, name="stage_2a")
@@ -94,9 +93,9 @@ def tile_picked_sub_mlp_silu_sub_e_kernel(tc, xT, w1, w2, gate, offs, pos1, pos2
         w1_scales = keep.tile([P, H], U8, name="w1_scales", align_bytes=64)
         w1_src = w1_raw[:].rearrange("p j (m u e) -> p u m j e", u=2, e=2)
         w1_dst = w1_bf[:].rearrange("p (u e m j) -> p u m j e", u=2, e=2, j=PACK)
-        nc.vector.tensor_copy(out=w1_dst[:, 0], in_=w1_src[:, 0])
-        nc.vector.tensor_copy(out=w1_dst[:, 1, 0:W1_VECTOR], in_=w1_src[:, 1, 0:W1_VECTOR])
-        nc.scalar.copy(out=w1_dst[:, 1, W1_VECTOR:P], in_=w1_src[:, 1, W1_VECTOR:P])
+        for u, share in enumerate(W1_VECTOR):
+            nc.vector.tensor_copy(out=w1_dst[:, u, 0:share], in_=w1_src[:, u, 0:share])
+            nc.scalar.copy(out=w1_dst[:, u, share:P], in_=w1_src[:, u, share:P])
         for u in range(2):
             cols = slice(u * H // 2, (u + 1) * H // 2)
             quantise(w1_codes[:, cols], w1_scales[:, cols], w1_bf[:, u * PACK * H // 2 : (u + 1) * PACK * H // 2])
@@ -107,15 +106,15 @@ def tile_picked_sub_mlp_silu_sub_e_kernel(tc, xT, w1, w2, gate, offs, pos1, pos2
         for j in range(2, PACK):
             nc.vector.tensor_copy(out=lo_slots[:, 0:P, j], in_=picked(j, 0, P))
             nc.scalar.activation(lo_slots[:, P : 2 * P, j], picked(j, P, 2 * P), COPY)
-            nc.scalar.activation(x_2[:, :, j], picked(j, 2 * P, 3 * P), COPY)
             nc.scalar.activation(stage_3[:, j, :], picked(j, 3 * P, S), COPY)
+            nc.scalar.activation(x_2[:, :, j], picked(j, 2 * P, 3 * P), COPY)
         quantise(x_codes[0][:], x_scales[0][:], x_lo[:, 0 : P * PACK])
         quantise(x_codes[1][:], x_scales[1][:], x_lo[:, P * PACK : 2 * P * PACK])
-        quantise(x_codes[2][:], x_scales[2][:], x_2[:].rearrange("p s j -> p (s j)"))
-        x_3 = turns.tile([P, P * PACK], BF16, name="x_3", align_bytes=64, offset=0)
+        x_3 = keep.tile([P, P * PACK], BF16, name="x_3", align_bytes=64)
         nc.vector.tensor_copy(
             out=x_3[:].rearrange("p (s i j) -> p s j i", i=4, j=PACK), in_=stage_3[:].rearrange("p j (s i) -> p s j i", i=4)
         )
+        quantise(x_codes[2][:], x_scales[2][:], x_2[:].rearrange("p s j -> p (s j)"))
 
         w2_bf = keep.tile([P, N * PACK], BF16, name="w2_bf", align_bytes=64)
         w2_codes = keep.tile([P, N], U32, name="w2_codes", align_bytes=64)

from contextlib import ExitStack

import concourse.mybir as mybir

K, T, D, S, V, H, N = 512, 1024, 3, 512, 256, 512, 256
FLOPS = 2 * S * (K * H + H * N) + 2 * D * N * V

F32 = mybir.dt.float32
BF16 = mybir.dt.bfloat16
U32 = mybir.dt.uint32
U16 = mybir.dt.uint16
U8 = mybir.dt.uint8
FP8X4 = mybir.dt.float8_e4m3fn_x4
SILU = mybir.ActivationFunctionType.Silu
COPY = mybir.ActivationFunctionType.Copy
MULT = mybir.AluOpType.mult
ADD = mybir.AluOpType.add

P = 128
PACK = 4
CHUNKS = S // P
W1_VECTOR = (96, 56)
WARM_ROWS = 32
SILU_CUTS = [(0, 128), (128, 256), (256, 384), (384, 448), (448, 512)]
Y_PASSES = [[(0, 256), (256, 384), (384, 448), (448, 512)], [(0, 256), (256, 384), (384, 512)]]
Y_COPIES = [[(0, 256, 4), (256, 448, 0), (448, 512, 6)], [(0, 384, 5), (384, 512, 7)]]
SCALAR_FETCHES = [(0, 1), (0, 2), (1, 0), (1, 1)]


def tile_picked_sub_mlp_silu_sub_e_kernel(tc, xT, w1, w2, gate, offs, pos1, pos2, pos3, out):
    nc = tc.nc
    with ExitStack() as ctx:
        keep = ctx.enter_context(tc.tile_pool(name="keep", bufs=1))
        psum = ctx.enter_context(tc.psum_pool(name="psum", bufs=1))

        offs_t = keep.tile([P, S // 16], U16, name="offs_t")
        pos_t = [keep.tile([P, V // 16], U16, name=f"pos_t{d}") for d in range(D)]
        x_rows = xT.rearrange("(p j) t -> p j t", j=PACK)
        x_first = keep.tile([P, 2, T], F32, name="x_first")
        nc.sync.dma_start(out=x_first[:], in_=x_rows[:, 0:2, :])
        nc.sync.dma_start(offs_t[:], offs)
        w1_raw = keep.tile([P, PACK, H], F32, name="w1_raw")
        nc.sync.dma_start(out=w1_raw[:], in_=w1.rearrange("(p j) c -> p j c", j=PACK))
        x_last = [keep.tile([P, T], F32, name=f"x_last{j}") for j in range(2)]
        for j in range(2):
            nc.sync.dma_start(out=x_last[j][:], in_=x_rows[:, 2 + j, :])
        planes = [x_first[:, 0, :], x_first[:, 1, :], x_last[0][:], x_last[1][:]]
        w2_raw = keep.tile([P, PACK, N], F32, name="w2_raw")
        nc.sync.dma_start(out=w2_raw[:], in_=w2.rearrange("(p j) n -> p j n", j=PACK))
        gate_t = keep.tile([P, D, V], F32, name="gate_t")
        nc.sync.dma_start(out=gate_t[:], in_=gate[:, 0:P, :].rearrange("d p v -> p d v"))
        for d, pos in enumerate((pos1, pos2, pos3)):
            nc.sync.dma_start(pos_t[d][:], pos)

        preload_in = keep.tile([P, 1], F32, name="preload_in")
        preload_out = keep.tile([P, 1], F32, name="preload_out")
        nc.gpsimd.memset(preload_in[:], 0.0)
        nc.scalar.activation(preload_out[:], preload_in[:], SILU)

        def quantise(codes, scales, values):
            nc.vector.quantize_mx(out=codes.bitcast(FP8X4), scales=scales, in_=values)

        def multiply(dst, w_codes, w_scales, m_codes, m_scales):
            nc.tensor.matmul_mx(
                out=dst,
                lhsT=w_codes.bitcast(FP8X4),
                lhsT_scale=w_scales,
                rhs=m_codes.bitcast(FP8X4),
                rhs_scale=m_scales,
                start=True,
                stop=True,
            )

        def picked(j, a, b):
            return planes[j].indirect(offs_t[:, a // 16 : b // 16])

        x_lo = keep.tile([P, 2 * P * PACK], BF16, name="x_lo", align_bytes=64)
        lo_slots = x_lo[:].rearrange("p (s j) -> p s j", j=PACK)
        x_2 = keep.tile([P, P, PACK], BF16, name="x_2", align_bytes=64)
        stage_2a = keep.tile([P, 2, P], F32, name="stage_2a")
        stage_3 = keep.tile([P, PACK, P], F32, name="stage_3")
        x_codes = [keep.tile([P, P], U32, name=f"x_codes{c}", align_bytes=64) for c in range(CHUNKS)]
        x_scales = [keep.tile([P, P], U8, name=f"x_scales{c}", align_bytes=64) for c in range(CHUNKS)]

        for j in range(2):
            nc.vector.tensor_copy(out=lo_slots[:, :, j], in_=picked(j, 0, 2 * P))
            nc.scalar.activation(stage_2a[:, j, :], picked(j, 2 * P, 3 * P), COPY)
            nc.scalar.activation(stage_3[:, j, :], picked(j, 3 * P, S), COPY)
        nc.vector.tensor_copy(out=x_2[:, :, 0:2], in_=stage_2a[:].rearrange("p j s -> p s j"))

        w1_bf = keep.tile([P, PACK * H], BF16, name="w1_bf", align_bytes=64)
        w1_codes = keep.tile([P, H], U32, name="w1_codes", align_bytes=64)
        w1_scales = keep.tile([P, H], U8, name="w1_scales", align_bytes=64)
        w1_src = w1_raw[:].rearrange("p j (m u e) -> p u m j e", u=2, e=2)
        w1_dst = w1_bf[:].rearrange("p (u e m j) -> p u m j e", u=2, e=2, j=PACK)
        for u, share in enumerate(W1_VECTOR):
            nc.vector.tensor_copy(out=w1_dst[:, u, 0:share], in_=w1_src[:, u, 0:share])
            nc.scalar.copy(out=w1_dst[:, u, share:P], in_=w1_src[:, u, share:P])
        for u in range(2):
            cols = slice(u * H // 2, (u + 1) * H // 2)
            quantise(w1_codes[:, cols], w1_scales[:, cols], w1_bf[:, u * PACK * H // 2 : (u + 1) * PACK * H // 2])
        warm_ps = psum.tile([WARM_ROWS, H], F32, name="warm_ps", tag="bank4")
        for width in (P, H, H):
            multiply(warm_ps[:, 0:width], w1_codes[:, 0:WARM_ROWS], w1_scales[:, 0:WARM_ROWS], w1_codes[:, 0:width], w1_scales[:, 0:width])

        for j in range(2, PACK):
            nc.vector.tensor_copy(out=lo_slots[:, 0:P, j], in_=picked(j, 0, P))
            nc.scalar.activation(lo_slots[:, P : 2 * P, j], picked(j, P, 2 * P), COPY)
            nc.scalar.activation(stage_3[:, j, :], picked(j, 3 * P, S), COPY)
            nc.scalar.activation(x_2[:, :, j], picked(j, 2 * P, 3 * P), COPY)
        quantise(x_codes[0][:], x_scales[0][:], x_lo[:, 0 : P * PACK])
        quantise(x_codes[1][:], x_scales[1][:], x_lo[:, P * PACK : 2 * P * PACK])
        x_3 = keep.tile([P, P * PACK], BF16, name="x_3", align_bytes=64)
        nc.vector.tensor_copy(
            out=x_3[:].rearrange("p (s i j) -> p s j i", i=4, j=PACK), in_=stage_3[:].rearrange("p j (s i) -> p s j i", i=4)
        )
        quantise(x_codes[2][:], x_scales[2][:], x_2[:].rearrange("p s j -> p (s j)"))

        w2_bf = keep.tile([P, N * PACK], BF16, name="w2_bf", align_bytes=64)
        w2_codes = keep.tile([P, N], U32, name="w2_codes", align_bytes=64)
        w2_scales = keep.tile([P, N], U8, name="w2_scales", align_bytes=64)
        w2_src = w2_raw[:].rearrange("p j (c i) -> p c j i", i=4)
        w2_dst = w2_bf[:].rearrange("p (c i j) -> p c j i", i=4, j=PACK)
        groups = N // 4
        nc.vector.tensor_copy(out=w2_dst[:, 0 : groups // 2], in_=w2_src[:, 0 : groups // 2])
        quantise(x_codes[3][:], x_scales[3][:], x_3[:])
        nc.vector.tensor_copy(out=w2_dst[:, groups // 2 :], in_=w2_src[:, groups // 2 :])

        h_bf = [keep.tile([P, b - a, PACK], BF16, name=f"h_bf{a}", align_bytes=64) for a, b in SILU_CUTS]
        h_codes = keep.tile([P, S], U32, name="h_codes", align_bytes=64)
        h_scales = keep.tile([P, S], U8, name="h_scales", align_bytes=64)
        h_pairs = keep.tile([P, 2, P, 2], BF16, name="h_pairs")
        for u, bank in enumerate((0, 7)):
            pair_ps = psum.tile([P, 2, P], F32, name=f"pair_ps{u}", tag=f"bank{bank}")
            for e in range(2):
                cols = slice((2 * u + e) * P, (2 * u + e + 1) * P)
                multiply(pair_ps[:, e, :], w1_codes[:, cols], w1_scales[:, cols], x_codes[0][:], x_scales[0][:])
            nc.scalar.activation(h_pairs[:, u], pair_ps[:].rearrange("p e s -> p s e"), SILU)
        nc.vector.tensor_copy(out=h_bf[0][:].rearrange("p s (u e) -> p s u e", e=2), in_=h_pairs[:].rearrange("p u s e -> p s u e"))
        for c in range(1, CHUNKS):
            h_ps = psum.tile([P, PACK, P], F32, name=f"h_ps{c}", tag=f"bank{c}")
            for t in range(PACK):
                cols = slice(t * P, (t + 1) * P)
                multiply(h_ps[:, t, :], w1_codes[:, cols], w1_scales[:, cols], x_codes[c][:], x_scales[c][:])
            for cut, (a, b) in enumerate(SILU_CUTS):
                if a // P == c:
                    nc.scalar.activation(h_bf[cut][:], h_ps[:, :, a - c * P : b - c * P].rearrange("p t s -> p s t"), SILU)

        y_t = [keep.tile([P, S], F32, name=f"y_t{half}") for half in range(2)]
        y_ps = [
            {a: psum.tile([P, b - a], F32, name=f"y_ps{half}_{a}", tag=f"bank{bank}") for a, b, bank in Y_COPIES[half]}
            for half in range(2)
        ]
        for cut, (cut_a, cut_b) in enumerate(SILU_CUTS):
            if cut == 0:
                quantise(w2_codes[:], w2_scales[:], w2_bf[:])
            quantise(h_codes[:, cut_a:cut_b], h_scales[:, cut_a:cut_b], h_bf[cut][:].rearrange("p s t -> p (s t)"))
            for half in range(2):
                cols = slice(half * P, (half + 1) * P)
                for a, b in Y_PASSES[half]:
                    if b == cut_b:
                        base = max(start for start in y_ps[half] if start <= a)
                        dst = y_ps[half][base][:, a - base : b - base]
                        multiply(dst, w2_codes[:, cols], w2_scales[:, cols], h_codes[:, a:b], h_scales[:, a:b])
        for half in range(2):
            for a, b, bank in Y_COPIES[half]:
                engine_copy = nc.vector.tensor_copy if half == 1 and b < S else nc.scalar.copy
                engine_copy(out=y_t[half][:, a:b], in_=y_ps[half][a][:])

        def neighbours(half, d, a, b):
            return y_t[half][:].indirect(pos_t[d][:, a // 16 : b // 16])

        term = [[keep.tile([P, V], F32, name=f"term{half}{d}") for d in range(D)] for half in range(2)]
        fetched = {pair: keep.tile([P, V], F32, name=f"fetched{pair[0]}{pair[1]}") for pair in SCALAR_FETCHES}
        partial = [keep.tile([P, V], F32, name=f"partial{half}") for half in range(2)]
        for half, d in SCALAR_FETCHES:
            nc.scalar.activation(fetched[half, d][:], neighbours(half, d, 0, V), COPY)

        def weigh(half, d, a=0, b=V):
            values = fetched[half, d][:, a:b] if (half, d) in fetched else neighbours(half, d, a, b)
            nc.vector.tensor_tensor(term[half][d][:, a:b], values, gate_t[:, d, a:b], MULT)

        def finish(half, d, cuts):
            result = keep.tile([P, V], F32, name=f"result{half}")
            for a, b in cuts:
                nc.vector.tensor_tensor(result[:, a:b], partial[half][:, a:b], term[half][d][:, a:b], ADD)
            nc.sync.dma_start(out=out[half * P : (half + 1) * P, :], in_=result[:])

        column_halves = [(0, V // 2), (V // 2, V)]
        weigh(0, 0)
        weigh(1, 2)
        weigh(0, 1)
        weigh(0, 2)
        nc.vector.tensor_tensor(partial[0][:], term[0][0][:], term[0][1][:], ADD)
        weigh(1, 0)
        finish(0, 2, [(0, V)])
        nc.vector.tensor_tensor(partial[1][:], term[1][2][:], term[1][0][:], ADD)
        for a, b in column_halves:
            weigh(1, 1, a, b)
        finish(1, 1, column_halves)
